import numpy as np, ml_dtypes
CORES = [78,86,94,102,110,118]
N = 6
import mx_ref
BF = ml_dtypes.bfloat16
def cols(t, e):
    v = np.concatenate([t.reshape(128, -1, 4), np.zeros((128, 1, 4), BF)], axis=1)
    return np.ascontiguousarray(v[:, e]).reshape(128, -1)
def decode(q):
    o = []
    for b in range(4):
        e = np.zeros((128, 128, 4), np.float32); e[np.arange(128), np.arange(128), b] = 1
        o.append(mx_ref.matmul(mx_ref.quantize(e.reshape(128, 512).astype(BF)), q))
    return np.stack(o, axis=2).reshape(128, -1)
def f(rng, *shape):
    return mx_ref.flush((rng.standard_normal(shape, dtype=np.float32) * np.exp2(rng.integers(-2, 3, shape[:-1] + (1,)))).astype(BF))
def wide(rng, *shape, cols=0):
    v = rng.standard_normal(shape, dtype=np.float32) * np.exp2(rng.integers(-12, 13, shape)).astype(np.float32)
    if cols: v *= np.repeat(np.exp2(rng.integers(-cols, cols + 1, shape[:-2] + (1, shape[-1] // 4))) * (rng.random(shape[:-2] + (1, shape[-1] // 4)) > 0.0625), 4, axis=-1).astype(np.float32)
    return mx_ref.flush(v.astype(BF))
T, K = 512, 160
def setup_inputs(rng):
    u = np.zeros((N, 128, 512), BF); u[:, :, :4] = f(rng, N, 128, 4)
    return {"gr": f(rng, N, 128, 4 * T), "u": u}
def raised(rng, chosen):
    d = setup_inputs(rng)
    for r in range(N):
        g = d["gr"][r].astype(np.float32).reshape(128, T, 4)
        sign = np.where(d["u"][r][:, :4].astype(np.float32) < 0, -1, 1).reshape(128, 1, 4) * rng.choice([-1, 1], K).reshape(1, K, 1)
        v = g * np.float32(2.0 ** -8)
        v[:, chosen[r]] = np.abs(g[:, chosen[r]]) * sign
        d["gr"][r] = mx_ref.flush(v.reshape(128, 4 * T).astype(BF))
    return d
def setup_inputs_same(rng):
    d = raised(rng, [rng.permutation(T)[:K]] * N)
    k = rng.permutation(np.concatenate([[12, -12, -11], rng.integers(-12, 13, N - 3)]))
    d["gr"] = mx_ref.flush((d["gr"].astype(np.float32) * np.exp2(k).astype(np.float32).reshape(N, 1, 1)).astype(BF))
    return d
def setup_inputs_apart(rng):
    p = rng.permutation(T)
    return raised(rng, [p[(r * K + np.arange(K)) % T] for r in range(N)])
def setup_inputs_ties(rng):
    d = setup_inputs(rng); n = T // 11
    for r in range(N):
        p = rng.permutation(T)[:11 * n]
        e = np.full(T, -1); e[p] = np.repeat(np.arange(n), 11)
        s = rng.choice([-1, 1], (n, 11)); s[:, 0] = 1; s[:, 1] = -1
        sign = np.ones(T, np.float32); sign[p] = s.reshape(-1)
        d["gr"][r] = (cols(d["gr"][r], e).astype(np.float32).reshape(128, T, 4) * sign.reshape(1, T, 1)).reshape(128, 4 * T).astype(BF)
    return d
def setup_inputs_few(rng):
    d = setup_inputs(rng); p = rng.permutation(N)
    d["u"][p[0]] = 0
    sign = rng.choice([-1, 1], (128, 1, 4))
    d["u"][p[1]][:, :4] = (sign * rng.uniform(1, 4, (128, 1, 4)) * 2.0 ** 28).reshape(128, 4).astype(BF)
    d["gr"][p[1]] = (sign * rng.choice([-1, 1], (1, T, 1)) * rng.uniform(1, 4, (128, T, 4)) * 2.0 ** 28).reshape(128, 4 * T).astype(BF)
    for r in p[2:2 + N // 2]:
        k = rng.permutation(T)[:rng.integers(1, K)]
        e = np.full(T, -1); e[k] = k
        d["gr"][r] = cols(d["gr"][r], e)
    return d
def setup_inputs_spread(rng):
    d = setup_inputs(rng); d["gr"] = wide(rng, N, 128, 4 * T, cols=8); return d
def check_inputs(d):
    return ["u"] if (d["u"][:, :, 4:].astype(np.float32) != 0).any() else []
def reference(gr, u):
    acc = np.zeros((128, T, 4), np.float32); nb = np.zeros((N, K), np.float32); sc = np.zeros((N, 1, K), np.float32)
    er = gr.astype(np.float32).reshape(N, 128, T, 4)
    for s in range(N):
        score = np.abs(mx_ref.matmul(mx_ref.quantize(u[s]), mx_ref.quantize(gr[s]))[0]) + np.float32(0.0)
        e = np.argsort(-score, kind="stable")[:K]
        v = decode(mx_ref.quantize(cols(gr[s], e))).reshape(128, K, 4)
        acc[:, e] = acc[:, e] + v
        er[s][:, e] = er[s][:, e] - v
        nb[s] = e
        sc[s, 0] = score[e]
    return {"acc": np.stack([acc.reshape(128, 4 * T)] * N), "er": er.reshape(N, 128, 4 * T), "nb": np.stack([nb] * N), "sc": sc}

@@ -1,0 +1,368 @@
+from concourse.bass import DstId, RemoteDMATransfer
+from concourse.mybir import dt, AluOpType, AxisListType, ActivationFunctionType
+
+N, TC, K = 6, 512, 160
+W = 8 + N * K
+LS = 24
+
+F, B, I, U, C8, P8 = "float32", "bfloat16", "int32", "uint16", "float8_e4m3fn_x4", "uint8"
+SCRATCH = {
+    "U4": ("sbuf", [128, 16], B), "UT": ("sbuf", [128, 512], B),
+    "UQ": ("sbuf", [128, 128], C8), "UP": ("sbuf", [128, 128], P8),
+    "GR": ("sbuf", [128, 2048], B), "GQ": ("sbuf", [128, 512], C8), "GP": ("sbuf", [128, 512], P8),
+    "ON": ("sbuf", [128, 516], B), "MM": ("sbuf", [128, 516], B),
+    "EQ": ("sbuf", [128, 512], C8), "EP": ("sbuf", [128, 512], P8),
+    "PS": ("psum", [128, 4096], F),
+    "SR": ("sbuf", [128, 512], F), "SL": ("sbuf", [128, 512], F), "SCO": ("sbuf", [128, 4], F),
+    "CM": ("sbuf", [128, 2560], B), "CJ": ("sbuf", [128, 1920], B), "CN": ("sbuf", [128, 4], F),
+    "OFF": ("sbuf", [128, 8], U), "DD": ("sbuf", [128, 128], F), "WW": ("sbuf", [128, 1056], F),
+    "TT": ("sbuf", [128, 448], F), "XX": ("sbuf", [128, 32], F), "ZZ": ("sbuf", [128, 80], F),
+    "RM": ("sbuf", [128, 80], F), "SC": ("sbuf", [128, 80], F),
+    "LT": ("sbuf", [128, 40], U), "LIN": ("sbuf", [128, N * LS], U),
+    "CG": ("sbuf", [128, 4 * K], B), "RC": ("sbuf", [128, N * K], C8), "RP": ("sbuf", [128, N * K], P8),
+    "DF": ("sbuf", [128, 4 * K], F), "ER": ("sbuf", [128, 2048], F), "Y": ("sbuf", [128, 4 * W], F),
+    "LR": ("sbuf", [128, 544], F), "KC": ("sbuf", [128, N * K], F), "PR": ("sbuf", [128, 192], F),
+    "T2": ("sbuf", [128, 288], F), "PL": ("sbuf", [128, 16 * N], U), "TL": ("sbuf", [128, 1056], F),
+    "LL": ("sbuf", [128, 32], U), "AC": ("sbuf", [128, 2048], F), "IO": ("sbuf", [128, 512], F),
+    "NB": ("sbuf", [128, N * K], F), "SO": ("sbuf", [128, K], F),
+    "VI": ("sbuf", [128, 32], I), "VJ": ("sbuf", [128, 32], I), "UL": ("sbuf", [128, 32], U),
+    "V2": ("sbuf", [128, 2], I), "CI": ("sbuf", [128, 32], I), "CF": ("sbuf", [128, 64], F),
+    "SE": ("sbuf", [128, 8], U), "D0": ("sbuf", [128, 128], F), "R0": ("sbuf", [128, 80], F),
+}
+_EV = ["v", "a", "t", "ld_u", "ld_g0", "ld_g1", "on", "ul", "io1", "io2", "io3", "io4", "io5", "io6", "mst", "ut", "uq",
+       "gq0", "gq1", "ms0", "ms1", "sr", "sco", "sl", "cm0", "cm1", "cm2", "cn", "er0", "er1", "xx", "za", "lt",
+       "ga", "lst", "qc", "df", "erx", "so", "nb", "add", "ll", "fv0", "fv1", "fa0", "fa1", "st", "sent"]
+SEMAPHORES = _EV + ["mm%d" % n for n in range(N)] + ["vc%d" % n for n in range(N)] \
+    + ["li%d" % s for s in range(N)] + ["ar%d" % s for s in range(N)]
+
+
+def tracked(q, T, name):
+    tot, pend = {}, {}
+
+    def rec(ins, ev=None):
+        e = ev or name
+        ins.then_inc(T.sem[e], 1)
+        tot[e] = tot.get(e, 0) + 1
+        pend[e] = tot[e]
+
+    def sync():
+        for e in list(pend):
+            q.wait_ge(T.sem[e], pend[e])
+        pend.clear()
+    return rec, sync
+
+
+def rank_program(g, core, T, topo):
+    r = T.rank_of(core)
+    if r is None:
+        return
+    A, AF = AluOpType, ActivationFunctionType
+    v, a, t, sy = g.vector, g.scalar, g.tensor, g.sync
+    S = T.sem
+    vr, vsync = tracked(v, T, "v")
+    ar, async_ = tracked(a, T, "a")
+    order = [r] + [s for s in range(N) if s != r]
+    turn = {s: n for n, s in enumerate(order)}
+
+    def ts(out, in0, s1, s2, op0, op1=None, ev=None):
+        if op1 is None:
+            vr(v.tensor_scalar(out, in0, s1, None, op0), ev)
+        else:
+            vr(v.tensor_scalar(out, in0, s1, s2, op0, op1), ev)
+
+    def tt(out, x, y, op, ev=None):
+        vr(v.tensor_tensor(out, x, y, op), ev)
+
+    sy.dma_start(T.U4[:, 0:4], T.u[:, 0:4]).then_inc(S.ld_u, 16)
+    sy.dma_start(T.GR[:, 0:1024], T.gr[:, 0:1024]).then_inc(S.ld_g0, 16)
+    a.dma_start(T.GR[:, 1024:2048], T.gr[:, 1024:2048]).then_inc(S.ld_g1, 16)
+
+    g.iota(T.VI[:], [[0, 32]], 0, 1).then_inc(S.io1, 1)
+    g.iota(T.V2[:], [[128, 2]], 0, 1).then_inc(S.io2, 1)
+    g.iota(T.D0[:], [[0, 2], [128, 4], [1, 16]], 0, 0, allow_small_or_imprecise_dtypes=True).then_inc(S.io3, 1)
+    g.wait_ge(S.on, 1)
+    g.affine_select(T.MM[:], T.ON[:], [[-1, 516]], A.is_equal, 0.0, 3, 4).then_inc(S.mst, 1)
+    g.iota(T.R0[:], [[0, 10], [1, 8]], 0, 0, allow_small_or_imprecise_dtypes=True).then_inc(S.io4, 1)
+    g.iota(T.KC[:], [[1, N * K]], 8, 0, allow_small_or_imprecise_dtypes=True).then_inc(S.io5, 1)
+    g.wait_ge(S.sr, 2)
+    g.affine_select(T.SL[:], T.SR[:], [[0, 4], [-1, 128]], A.is_gt, -1.0, 0, 1).then_inc(S.sl, 1)
+    g.iota(T.IO[:], [[1, 512]], 0, 0, allow_small_or_imprecise_dtypes=True).then_inc(S.io6, 1)
+
+    vr(v.memset(T.ON[:], 1.0), "on")
+    v.wait_ge(S.io1, 1)
+    ts(T.VJ[:], T.VI[:], 3, None, A.bitwise_and)
+    vsync()
+    vr(v.tensor_copy(T.UL[:], T.VJ[:]), "ul")
+    v.wait_ge(S.io2, 1)
+    ci = lambda k: T.CI[:, 2 * k:2 * k + 2]
+    cf = lambda k: T.CF[:, 2 * k:2 * k + 2]
+    ts(ci(0), T.V2[:], 14, None, A.bitwise_and)
+    ts(ci(1), T.V2[:], 12, None, A.bitwise_and)
+    ts(ci(2), T.V2[:], 1, None, A.bitwise_and)
+    ts(ci(3), T.V2[:], 1, 1, A.arith_shift_right, A.bitwise_and)
+    ts(ci(4), T.V2[:], 4, 1, A.arith_shift_right, A.bitwise_and)
+    ts(ci(5), T.V2[:], 128, None, A.bitwise_and)
+    ts(ci(6), T.V2[:], 15, None, A.bitwise_and)
+    ts(ci(7), T.V2[:], 112, None, A.bitwise_and)
+    vsync()
+    vr(v.tensor_copy(T.CF[:, 0:16], T.CI[:, 0:16]))
+    vr(v.memset(T.WW[:, 0:160], 0.0))
+    vr(v.memset(T.WW[:, 512:704], 0.0))
+    vr(v.memset(T.TT[:, 352:448], 0.0))
+    vr(v.memset(T.T2[:, 192:288], 0.0))
+    vsync()
+    tt(cf(8), cf(3), cf(4), A.mult)
+    tt(cf(9), cf(2), cf(4), A.mult)
+    tt(cf(10), cf(6), cf(4), A.subtract)
+    vsync()
+    ts(cf(11), cf(1), 8.0, None, A.mult)
+    ts(cf(12), cf(2), 16.0, None, A.mult)
+    ts(cf(13), cf(3), 192.0, None, A.mult)
+    ts(cf(14), cf(4), 160.0, None, A.mult)
+    ts(cf(15), cf(8), 352.0, None, A.mult)
+    ts(cf(16), cf(0), 16.0, None, A.mult)
+    ts(cf(17), cf(2), 544.0, None, A.mult)
+    ts(cf(18), cf(4), 512.0, None, A.mult)
+    ts(cf(19), cf(9), 1056.0, None, A.mult)
+    ts(cf(20), cf(2), 48.0, None, A.mult)
+    ts(cf(21), cf(4), 16.0, None, A.mult)
+    ts(cf(22), cf(9), 64.0, None, A.mult)
+    ts(cf(23), cf(5), 2.0, None, A.mult)
+    ts(cf(24), cf(10), 0.0, 9.0, A.max, A.min)
+    v.wait_ge(S.io3, 1)
+    ts(T.DD[:], T.D0[:], T.CF[:, 14:15], None, A.add)
+    v.wait_ge(S.io4, 1)
+    ts(T.RM[:], T.R0[:], 1.0, None, A.min)
+    vsync()
+    tt(cf(25), cf(5), cf(11), A.add)
+    tt(cf(26), cf(12), cf(13), A.add)
+    tt(cf(27), cf(14), cf(15), A.subtract)
+    tt(cf(28), cf(23), cf(16), A.add)
+    tt(cf(29), cf(17), cf(18), A.add)
+    tt(cf(30), cf(20), cf(21), A.add)
+    tt(cf(31), cf(16), cf(22), A.subtract)
+    ts(T.SE[:, 2:4], cf(24), 8.0, 7.0, A.mult, A.add)
+    vsync()
+    tt(cf(11), cf(25), cf(26), A.add)
+    tt(cf(17), cf(28), cf(29), A.add)
+    tt(T.SE[:, 6:8], cf(30), cf(31), A.add)
+    vsync()
+    tt(T.SE[:, 0:2], cf(11), cf(27), A.add)
+    tt(T.SE[:, 4:6], cf(17), cf(19), A.subtract)
+    v.wait_ge(S.mst, 1)
+    for b in range(4):
+        vr(v.quantize_mx(T.EQ[:, 128 * b:128 * b + 128], T.EP[:, 128 * b:128 * b + 128], T.MM[:, 3 - b:515 - b]))
+    vr(v.memset(T.LR[:], 0.0))
+    for b in range(4):
+        vr(v.memset(T.Y[:, W * b:W * b + 8], 0.0), "on")
+
+    a.wait_ge(S.ld_u, 16)
+    a.wait_ge(S.ul, 1)
+    ar(a.activation(T.UT[:], T.U4[:, 0:4].indirect(T.UL[:, 0:32]), AF.Copy), "ut")
+    v.wait_ge(S.ut, 1)
+    vr(v.quantize_mx(T.UQ[:], T.UP[:], T.UT[:]), "uq")
+    for h in range(2):
+        v.wait_ge(S["ld_g%d" % h], 16)
+        c = slice(256 * h, 256 * h + 256)
+        vr(v.quantize_mx(T.GQ[:, c], T.GP[:, c], T.GR[:, 1024 * h:1024 * h + 1024]), "gq%d" % h)
+    t.wait_ge(S.uq, 1)
+    for h in range(2):
+        t.wait_ge(S["gq%d" % h], 1)
+        c = slice(256 * h, 256 * h + 256)
+        t.matmul_mx(T.PS[:, 512 * h:512 * h + 256], T.UQ[:], T.UP[:], T.GQ[:, c], T.GP[:, c], True, True).then_inc(S["ms%d" % h], 1)
+    for b in range(4):
+        c = slice(128 * b, 128 * b + 128)
+        t.matmul_mx(T.PS[:, 2048 + 512 * b:2176 + 512 * b], T.GQ[:, c], T.GP[:, c], T.UQ[:], T.UP[:], True, True).then_inc(S.t, 1)
+    for h in range(2):
+        a.wait_ge(S["ms%d" % h], 1)
+        ar(a.activation(T.SR[:, 256 * h:256 * h + 256], T.PS[:, 512 * h:512 * h + 256], AF.Abs), "sr")
+    a.wait_ge(S.t, 4)
+    ar(a.activation(T.SCO[:], T.PS[:, 2048:4096:512], AF.Abs), "sco")
+    for k in range(2):
+        ar(a.activation(T.ER[:, 512 * k:512 * k + 512], T.GR[:, 512 * k:512 * k + 512], AF.Copy), "er0")
+
+    v.wait_ge(S.sr, 2)
+    v.wait_ge(S.sco, 1)
+
+    def before(b):
+        ev = "cm%d" % b if b < 3 else None
+        z = 640 * b
+        s = T.SCO[:, b:b + 1]
+        if b:
+            ts(T.CM[:, z:z + 128 * b], T.SR[:, 0:128 * b], s, None, A.is_ge, ev=ev)
+        ts(T.CM[:, z + 128 * b:z + 512], T.SR[:, 128 * b:512], s, None, A.is_gt, ev=ev)
+
+    def equal(b):
+        ev = "cm%d" % b if b < 3 else None
+        ts(T.CM[:, 640 * b + 512:640 * b + 640], T.SL[:, 128 * b:128 * b + 128], T.SCO[:, b:b + 1], None, A.is_equal, ev=ev)
+    before(0)
+    before(1)
+    v.wait_ge(S.sl, 1)
+    equal(0)
+    equal(1)
+    for b in (2, 3):
+        before(b)
+        equal(b)
+    for b in range(3):
+        a.wait_ge(S["cm%d" % b], 3 if b else 2)
+        ar(a.activation(T.CJ[:, 640 * b:640 * b + 640], T.CM[:, 640 * b:640 * b + 640], AF.Copy, accum_out=T.CN[:, b:b + 1]), "cn")
+    vsync()
+    vr(v.tensor_reduce(T.CN[:, 3:4], T.CM[:, 1920:2560], AxisListType.X, A.add))
+    vsync()
+    v.wait_ge(S.cn, 3)
+
+    ts(T.OFF[:, 0:4], T.CN[:], 0.0, None, A.add)
+    ts(T.OFF[:, 4:8], T.CN[:], 528.0, None, A.add)
+    vsync()
+    vr(v.tensor_copy(T.WW[:, 0:1056].indirect(T.OFF[:, 0:8]), T.DD[:]))
+    vsync()
+    vr(v.transpose(T.TT[:, 0:160], T.WW[:, 0:160]))
+    vr(v.transpose(T.TT[:, 160:352], T.WW[:, 512:704]))
+    vsync()
+    vr(v.tensor_copy(T.XX[:], T.TT[:, 0:448].indirect(T.SE[:, 0:2])), "xx")
+    for k in (2, 3):
+        ar(a.activation(T.ER[:, 512 * k:512 * k + 512], T.GR[:, 512 * k:512 * k + 512], AF.Copy), "er0")
+    vsync()
+    a.wait_ge(S.xx, 1)
+    vr(v.tensor_copy(T.ZZ[:, 0:80:4], T.XX[:, 0:20]))
+    for p in (0, 64):
+        vr(v.tensor_copy(T.ZZ[64 - p:128 - p, 2:80:4], T.XX[p:p + 64, 0:20]))
+    for d in (1, 3):
+        for p in range(4):
+            o = 32 * (p ^ d)
+            dst, src = T.ZZ[o:o + 32, d:80:4], T.XX[32 * p:32 * p + 32, 0:20]
+            if d == 1 and p < 3:
+                vr(v.tensor_copy(dst, src))
+            else:
+                ar(a.activation(dst, src, AF.Copy), "za")
+    vsync()
+    v.wait_ge(S.za, 5)
+    vr(v.tensor_tensor_scan(T.SC[:], T.RM[:], T.ZZ[:], 0.0, A.mult, A.add))
+    vsync()
+    num = T.SC[:, 7:80:8]
+    for k in (2, 3, 0, 1):
+        ts(T.LT[:, 10 * k:10 * k + 10], num, 4.0, float(k), A.mult, A.add, ev="lt" if k > 1 else None)
+    lo = LS * r
+    vr(v.tensor_copy(T.LIN[:, lo:lo + 16], T.SC[:].indirect(T.SE[:, 2:3])), "lst")
+    vsync()
+    ts(T.LIN[:, lo + 12:lo + 22], num, 0.0, None, A.add, ev="lst")
+    ts(T.LIN[:, lo + 22:lo + 24], T.SC[:, 7:23:8], 0.0, None, A.add, ev="lst")
+
+    a.wait_ge(S.lt, 2)
+    for k in (2, 3):
+        ar(a.activation(T.CG[:, k:4 * K:4], T.GR[:].indirect(T.LT[:, 10 * k:10 * k + 10]), AF.Copy), "ga")
+    for k in (0, 1):
+        vr(v.tensor_copy(T.CG[:, k:4 * K:4], T.GR[:].indirect(T.LT[:, 10 * k:10 * k + 10])))
+    vsync()
+    v.wait_ge(S.ga, 2)
+    own = slice(K * r, K * r + K)
+    vr(v.quantize_mx(T.RC[:, own], T.RP[:, own], T.CG[:]), "qc")
+
+    others = [T.cores[s] for s in order[1:]]
+    mask = topo.mask(core, others[0])
+    ne = len(topo.engines(core, others[0]))
+    ids = [DstId(rid=topo.addr(d)[0], pnc=topo.addr(d)[1]) for d in others]
+
+    def send(src, sem):
+        g.remote_dma_fused([RemoteDMATransfer(dst_ids=ids, dma_engine_mask=mask, remote_sem=S[sem], srcs=[src], dsts=[src] * len(ids))],
+                           local_sem=S.sent)
+    g.wait_ge(S.lst, 3)
+    send(T.LIN[:, lo:lo + LS], "li%d" % r)
+    g.wait_ge(S.qc, 1)
+    send(T.RC[:, own].bitcast(dt.uint8), "ar%d" % r)
+    send(T.RP[:, own], "ar%d" % r)
+
+    def decode(n):
+        s = order[n]
+        if n == 0:
+            t.wait_ge(S.qc, 1)
+            t.wait_ge(S.on, 5)
+            t.wait_ge(S.sr, 2)
+        else:
+            t.wait_ge(S["ar%d" % s], 2 * ne)
+            if n == 1:
+                t.wait_ge(S.sco, 1)
+            else:
+                t.wait_ge(S["vc%d" % (n - 2)], 4)
+        z = 2048 * (n % 2)
+        for b in range(4):
+            t.matmul_mx(T.PS[:, z + 512 * b:z + 512 * b + K], T.EQ[:, 128 * b:128 * b + 128], T.EP[:, 128 * b:128 * b + 128],
+                        T.RC[:, K * s:K * s + K], T.RP[:, K * s:K * s + K], True, True).then_inc(S["mm%d" % n], 1)
+
+    def unload(n):
+        s, z = order[n], 2048 * (n % 2)
+        a.wait_ge(S["mm%d" % n], 4)
+        for b in range(4):
+            o = W * b + 8 + K * s
+            ar(a.activation(T.Y[:, o:o + K], T.PS[:, z + 512 * b:z + 512 * b + K], AF.Copy), "vc%d" % n)
+    for n in range(N):
+        decode(n)
+
+    v.wait_ge(S.mm0, 4)
+    for b in range(4):
+        tt(T.DF[:, K * b:K * b + K], T.CG[:, b:4 * K:4], T.PS[:, 512 * b:512 * b + K], A.subtract, ev="df")
+    vsync()
+    v.wait_ge(S.er0, 4)
+    vr(v.tensor_copy(T.ER[:].indirect(T.LT[:, 0:40]), T.DF[:]), "erx")
+    sy.wait_ge(S.erx, 1)
+    sy.dma_start(T.er[:], T.ER[:]).then_inc(S.st, 16)
+
+    plain = lambda s: T.LIN[:, LS * s + 12:LS * s + 22]
+    a.wait_ge(S.lst, 3)
+    ar(a.activation(T.SO[:], T.SR[:].indirect(plain(r)), AF.Copy), "so")
+    sy.wait_ge(S.so, 1)
+    sy.dma_start(T.sc[:], T.SO[0:1, :]).then_inc(S.st, 16)
+    a.wait_ge(S.df, 4)
+    unload(0)
+    a.wait_ge(S.io6, 1)
+    for s in order:
+        if s != r:
+            a.wait_ge(S["li%d" % s], ne)
+        ar(a.activation(T.NB[:, K * s:K * s + K], T.IO[:].indirect(plain(s)), AF.Copy), "nb")
+    sy.wait_ge(S.nb, N)
+    sy.dma_start(T.nb[:], T.NB[0:1, :]).then_inc(S.st, 16)
+    for n in range(1, N):
+        unload(n)
+
+    v.wait_ge(S.io5, 1)
+    for s in range(N):
+        if s != r:
+            v.wait_ge(S["li%d" % s], ne)
+        if s:
+            vr(v.tensor_copy(T.PR[:], T.LR[:, 16:528].indirect(T.LIN[:, LS * s:LS * s + 12])))
+            vsync()
+        vr(v.tensor_copy(T.LR[:, 16:528].indirect(plain(s)), T.KC[:, K * s:K * s + K]))
+        if s:
+            vr(v.transpose(T.T2[:, 0:192], T.PR[:]))
+        vsync()
+        if s:
+            vr(v.tensor_copy(T.PL[:, 16 * s:16 * s + 16], T.T2[:].indirect(T.SE[:, 6:7])))
+    vr(v.transpose(T.TL[:, 0:512], T.LR[:, 16:528]))
+    vr(v.transpose(T.TL[:, 512:1056], T.LR[:, 0:544]))
+    vsync()
+    vr(v.tensor_copy(T.LL[:], T.TL[:].indirect(T.SE[:, 4:6])), "ll")
+
+    for s in range(1, N):
+        for k in ([0, 1] if s == 1 else [s]):
+            v.wait_ge(S["vc%d" % turn[k]], 4)
+        for b in range(4):
+            o = W * b + 8 + K * s
+            tt(T.Y[:, o:o + K], T.Y[:, W * b:o].indirect(T.PL[:, 16 * s:16 * s + 10]), T.Y[:, o:o + K], A.add,
+               ev="add" if s == N - 1 else None)
+        vsync()
+    a.wait_ge(S.add, 4)
+    a.wait_ge(S.ll, 1)
+    for h in range(2):
+        for b in range(4):
+            out = T.AC[:, 1024 * h + b:1024 * h + 1024:4]
+            win = T.Y[:, W * b:W * b + W].indirect(T.LL[:, 16 * h:16 * h + 16])
+            if b < 2:
+                vr(v.tensor_copy(out, win), "fv%d" % h)
+            else:
+                ar(a.activation(out, win, AF.Copy), "fa%d" % h)
+        sy.wait_ge(S["fv%d" % h], 2)
+        sy.wait_ge(S["fa%d" % h], 2)
+        sy.dma_start(T.acc[:, 1024 * h:1024 * h + 1024], T.AC[:, 1024 * h:1024 * h + 1024]).then_inc(S.st, 16)
+    vsync()
+    g.wait_ge(S.sent, 3 * ne)
+    sy.wait_ge(S.st, 80)

@@ -1,24 +1,25 @@
 from concourse.bass import DstId, RemoteDMATransfer
-from concourse.mybir import dt, AluOpType, AxisListType, ActivationFunctionType
+from concourse.mybir import dt, AluOpType, ActivationFunctionType
 
 N, TC, K = 6, 512, 160
 W = 8 + N * K
-LS = 24
+L = K // 16
+SHARE = [(2, 2, 1)] * N
 
 F, B, I, U, C8, P8 = "float32", "bfloat16", "int32", "uint16", "float8_e4m3fn_x4", "uint8"
 SCRATCH = {
     "U4": ("sbuf", [128, 16], B), "UT": ("sbuf", [128, 512], B),
     "UQ": ("sbuf", [128, 128], C8), "UP": ("sbuf", [128, 128], P8),
     "GR": ("sbuf", [128, 2048], B), "GQ": ("sbuf", [128, 512], C8), "GP": ("sbuf", [128, 512], P8),
-    "ON": ("sbuf", [128, 516], B), "MM": ("sbuf", [128, 516], B),
+    "ON": ("sbuf", [128, 640], B), "MM": ("sbuf", [128, 516], B),
     "EQ": ("sbuf", [128, 512], C8), "EP": ("sbuf", [128, 512], P8),
     "PS": ("psum", [128, 4096], F),
     "SR": ("sbuf", [128, 512], F), "SL": ("sbuf", [128, 512], F), "SCO": ("sbuf", [128, 4], F),
-    "CM": ("sbuf", [128, 2560], B), "CJ": ("sbuf", [128, 1920], B), "CN": ("sbuf", [128, 4], F),
+    "CM": ("sbuf", [128, 2560], B), "CN": ("sbuf", [128, 1280], B),
     "OFF": ("sbuf", [128, 8], U), "DD": ("sbuf", [128, 128], F), "WW": ("sbuf", [128, 1056], F),
     "TT": ("sbuf", [128, 448], F), "XX": ("sbuf", [128, 32], F), "ZZ": ("sbuf", [128, 80], F),
     "RM": ("sbuf", [128, 80], F), "SC": ("sbuf", [128, 80], F),
-    "LT": ("sbuf", [128, 40], U), "LIN": ("sbuf", [128, N * LS], U),
+    "LT": ("sbuf", [128, 40], U), "LIN": ("sbuf", [128, 16 * N], U), "SH": ("sbuf", [128, 16], U),
     "CG": ("sbuf", [128, 4 * K], B), "RC": ("sbuf", [128, N * K], C8), "RP": ("sbuf", [128, N * K], P8),
     "DF": ("sbuf", [128, 4 * K], F), "ER": ("sbuf", [128, 2048], F), "Y": ("sbuf", [128, 4 * W], F),
     "LR": ("sbuf", [128, 544], F), "KC": ("sbuf", [128, N * K], F), "PR": ("sbuf", [128, 192], F),
@@ -26,14 +27,14 @@ SCRATCH = {
     "LL": ("sbuf", [128, 32], U), "AC": ("sbuf", [128, 2048], F), "IO": ("sbuf", [128, 512], F),
     "NB": ("sbuf", [128, N * K], F), "SO": ("sbuf", [128, K], F),
     "VI": ("sbuf", [128, 32], I), "VJ": ("sbuf", [128, 32], I), "UL": ("sbuf", [128, 32], U),
-    "V2": ("sbuf", [128, 2], I), "CI": ("sbuf", [128, 32], I), "CF": ("sbuf", [128, 64], F),
+    "V2": ("sbuf", [128, 2], I), "CI": ("sbuf", [128, 16], I), "CF": ("sbuf", [128, 64], F),
     "SE": ("sbuf", [128, 8], U), "D0": ("sbuf", [128, 128], F), "R0": ("sbuf", [128, 80], F),
 }
 _EV = ["v", "a", "t", "ld_u", "ld_g0", "ld_g1", "on", "ul", "io1", "io2", "io3", "io4", "io5", "io6", "mst", "ut", "uq",
-       "gq0", "gq1", "ms0", "ms1", "sr", "sco", "sl", "cm0", "cm1", "cm2", "cn", "er0", "er1", "xx", "za", "lt",
-       "ga", "lst", "qc", "df", "erx", "so", "nb", "add", "ll", "fv0", "fv1", "fa0", "fa1", "st", "sent"]
-SEMAPHORES = _EV + ["mm%d" % n for n in range(N)] + ["vc%d" % n for n in range(N)] \
-    + ["li%d" % s for s in range(N)] + ["ar%d" % s for s in range(N)]
+       "gq0", "gq1", "ms0", "ms1", "sr", "sco", "sl", "er0", "xx", "za", "lt", "zw", "zl", "eq",
+       "ga", "lst", "qc", "df", "erx", "so", "nb", "add", "ll", "st", "sent", "pls", "hp", "hc"]
+SEMAPHORES = _EV + ["%s%d" % (e, n) for e in ("mm", "vc", "li", "ar", "pl") for n in range(N)] \
+    + ["%s%d" % (e, n) for e in ("fv", "fa") for n in range(4)]
 
 
 def tracked(q, T, name):
@@ -52,10 +53,48 @@ def tracked(q, T, name):
     return rec, sync
 
 
+def plan(T, topo, r):
+    core = T.cores[r]
+    others = [T.cores[(r + d) % N] for d in range(1, N)]
+    hs = [c for c in topo.cores_of(core) if c != core and all(topo.may_write(c, d) for d in others)]
+    hs.sort(key=lambda c: topo.die(c) == topo.die(core))
+    out, i = [], 0
+    for c, n in zip([core] + hs, SHARE[r]):
+        if n or c == core:
+            out.append((c, others[i:i + n]))
+        i += n
+    return others, out
+
+
+def ids_of(topo, cores):
+    return [DstId(rid=topo.addr(d)[0], pnc=topo.addr(d)[1]) for d in cores]
+
+
+def transfer(topo, src, cores, mask, sem):
+    return RemoteDMATransfer(dst_ids=ids_of(topo, cores), dma_engine_mask=mask, remote_sem=sem, srcs=[src], dsts=[src] * len(cores))
+
+
+def helper_program(g, core, T, topo):
+    S = T.sem
+    for r in range(N):
+        if topo.chip(T.cores[r]) != topo.chip(core):
+            continue
+        for c, dests in plan(T, topo, r)[1]:
+            if c != core:
+                continue
+            own = slice(K * r, K * r + K)
+            mask, ne = topo.mask(core, dests[0]), len(topo.engines(core, dests[0]))
+            nin = len(topo.engines(T.cores[r], core)) - len(topo.engines(T.cores[r], dests[0]))
+            for sem, src in (("hp", T.RP[:, own]), ("hc", T.RC[:, own].bitcast(dt.uint8))):
+                g.wait_ge(S[sem], nin)
+                g.remote_dma_fused([transfer(topo, src, dests, mask, S["ar%d" % r])], local_sem=S.sent)
+            g.wait_ge(S.sent, 2 * ne)
+
+
 def rank_program(g, core, T, topo):
     r = T.rank_of(core)
     if r is None:
-        return
+        return helper_program(g, core, T, topo)
     A, AF = AluOpType, ActivationFunctionType
     v, a, t, sy = g.vector, g.scalar, g.tensor, g.sync
     S = T.sem
@@ -80,13 +119,21 @@ def rank_program(g, core, T, topo):
     g.iota(T.VI[:], [[0, 32]], 0, 1).then_inc(S.io1, 1)
     g.iota(T.V2[:], [[128, 2]], 0, 1).then_inc(S.io2, 1)
     g.iota(T.D0[:], [[0, 2], [128, 4], [1, 16]], 0, 0, allow_small_or_imprecise_dtypes=True).then_inc(S.io3, 1)
-    g.wait_ge(S.on, 1)
-    g.affine_select(T.MM[:], T.ON[:], [[-1, 516]], A.is_equal, 0.0, 3, 4).then_inc(S.mst, 1)
     g.iota(T.R0[:], [[0, 10], [1, 8]], 0, 0, allow_small_or_imprecise_dtypes=True).then_inc(S.io4, 1)
-    g.iota(T.KC[:], [[1, N * K]], 8, 0, allow_small_or_imprecise_dtypes=True).then_inc(S.io5, 1)
+    g.wait_ge(S.on, 1)
+    g.affine_select(T.MM[:], T.ON[:, 0:516], [[-1, 516]], A.is_equal, 0.0, 3, 4).then_inc(S.mst, 1)
     g.wait_ge(S.sr, 2)
     g.affine_select(T.SL[:], T.SR[:], [[0, 4], [-1, 128]], A.is_gt, -1.0, 0, 1).then_inc(S.sl, 1)
+    g.iota(T.KC[:], [[1, N * K]], 8, 0, allow_small_or_imprecise_dtypes=True).then_inc(S.io5, 1)
     g.iota(T.IO[:], [[1, 512]], 0, 0, allow_small_or_imprecise_dtypes=True).then_inc(S.io6, 1)
+
+    a.wait_ge(S.on, 1)
+    for out, n, ev in ((T.WW[:, 0:160], 160, "zw"), (T.WW[:, 512:704], 192, "zw"), (T.TT[:, 352:448], 96, "zw"),
+                       (T.T2[:, 192:288], 96, "zl"), (T.LR[:], 544, "zl")):
+        ar(a.activation(out, T.ON[:, 0:n], AF.Copy, scale=0.0), ev)
+    a.wait_ge(S.ld_u, 16)
+    a.wait_ge(S.ul, 1)
+    ar(a.activation(T.UT[:], T.U4[:, 0:4].indirect(T.UL[:, 0:32]), AF.Copy), "ut")
 
     vr(v.memset(T.ON[:], 1.0), "on")
     v.wait_ge(S.io1, 1)
@@ -105,66 +152,36 @@ def rank_program(g, core, T, topo):
     ts(ci(6), T.V2[:], 15, None, A.bitwise_and)
     ts(ci(7), T.V2[:], 112, None, A.bitwise_and)
     vsync()
-    vr(v.tensor_copy(T.CF[:, 0:16], T.CI[:, 0:16]))
-    vr(v.memset(T.WW[:, 0:160], 0.0))
-    vr(v.memset(T.WW[:, 512:704], 0.0))
-    vr(v.memset(T.TT[:, 352:448], 0.0))
-    vr(v.memset(T.T2[:, 192:288], 0.0))
+    vr(v.tensor_copy(T.CF[:, 0:16], T.CI[:]))
     vsync()
     tt(cf(8), cf(3), cf(4), A.mult)
-    tt(cf(9), cf(2), cf(4), A.mult)
-    tt(cf(10), cf(6), cf(4), A.subtract)
-    vsync()
     ts(cf(11), cf(1), 8.0, None, A.mult)
     ts(cf(12), cf(2), 16.0, None, A.mult)
     ts(cf(13), cf(3), 192.0, None, A.mult)
     ts(cf(14), cf(4), 160.0, None, A.mult)
-    ts(cf(15), cf(8), 352.0, None, A.mult)
-    ts(cf(16), cf(0), 16.0, None, A.mult)
-    ts(cf(17), cf(2), 544.0, None, A.mult)
-    ts(cf(18), cf(4), 512.0, None, A.mult)
-    ts(cf(19), cf(9), 1056.0, None, A.mult)
-    ts(cf(20), cf(2), 48.0, None, A.mult)
-    ts(cf(21), cf(4), 16.0, None, A.mult)
-    ts(cf(22), cf(9), 64.0, None, A.mult)
-    ts(cf(23), cf(5), 2.0, None, A.mult)
-    ts(cf(24), cf(10), 0.0, 9.0, A.max, A.min)
     v.wait_ge(S.io3, 1)
     ts(T.DD[:], T.D0[:], T.CF[:, 14:15], None, A.add)
     v.wait_ge(S.io4, 1)
     ts(T.RM[:], T.R0[:], 1.0, None, A.min)
     vsync()
+    ts(cf(15), cf(8), 352.0, None, A.mult)
     tt(cf(25), cf(5), cf(11), A.add)
     tt(cf(26), cf(12), cf(13), A.add)
+    vsync()
     tt(cf(27), cf(14), cf(15), A.subtract)
-    tt(cf(28), cf(23), cf(16), A.add)
-    tt(cf(29), cf(17), cf(18), A.add)
-    tt(cf(30), cf(20), cf(21), A.add)
-    tt(cf(31), cf(16), cf(22), A.subtract)
-    ts(T.SE[:, 2:4], cf(24), 8.0, 7.0, A.mult, A.add)
+    tt(cf(28), cf(25), cf(26), A.add)
     vsync()
-    tt(cf(11), cf(25), cf(26), A.add)
-    tt(cf(17), cf(28), cf(29), A.add)
-    tt(T.SE[:, 6:8], cf(30), cf(31), A.add)
-    vsync()
-    tt(T.SE[:, 0:2], cf(11), cf(27), A.add)
-    tt(T.SE[:, 4:6], cf(17), cf(19), A.subtract)
-    v.wait_ge(S.mst, 1)
-    for b in range(4):
-        vr(v.quantize_mx(T.EQ[:, 128 * b:128 * b + 128], T.EP[:, 128 * b:128 * b + 128], T.MM[:, 3 - b:515 - b]))
-    vr(v.memset(T.LR[:], 0.0))
-    for b in range(4):
-        vr(v.memset(T.Y[:, W * b:W * b + 8], 0.0), "on")
+    tt(T.SE[:, 0:2], cf(28), cf(27), A.add)
 
-    a.wait_ge(S.ld_u, 16)
-    a.wait_ge(S.ul, 1)
-    ar(a.activation(T.UT[:], T.U4[:, 0:4].indirect(T.UL[:, 0:32]), AF.Copy), "ut")
     v.wait_ge(S.ut, 1)
     vr(v.quantize_mx(T.UQ[:], T.UP[:], T.UT[:]), "uq")
     for h in range(2):
         v.wait_ge(S["ld_g%d" % h], 16)
         c = slice(256 * h, 256 * h + 256)
         vr(v.quantize_mx(T.GQ[:, c], T.GP[:, c], T.GR[:, 1024 * h:1024 * h + 1024]), "gq%d" % h)
+    v.wait_ge(S.mst, 1)
+    for b in range(4):
+        vr(v.quantize_mx(T.EQ[:, 128 * b:128 * b + 128], T.EP[:, 128 * b:128 * b + 128], T.MM[:, 3 - b:515 - b]), "eq")
     t.wait_ge(S.uq, 1)
     for h in range(2):
         t.wait_ge(S["gq%d" % h], 1)
@@ -178,50 +195,55 @@ def rank_program(g, core, T, topo):
         ar(a.activation(T.SR[:, 256 * h:256 * h + 256], T.PS[:, 512 * h:512 * h + 256], AF.Abs), "sr")
     a.wait_ge(S.t, 4)
     ar(a.activation(T.SCO[:], T.PS[:, 2048:4096:512], AF.Abs), "sco")
-    for k in range(2):
+    for b in range(4):
+        ar(a.activation(T.Y[:, W * b:W * b + 8], T.ON[:, 0:8], AF.Copy, scale=0.0), "zl")
+    for k in range(4):
         ar(a.activation(T.ER[:, 512 * k:512 * k + 512], T.GR[:, 512 * k:512 * k + 512], AF.Copy), "er0")
 
     v.wait_ge(S.sr, 2)
     v.wait_ge(S.sco, 1)
 
     def before(b):
-        ev = "cm%d" % b if b < 3 else None
         z = 640 * b
         s = T.SCO[:, b:b + 1]
         if b:
-            ts(T.CM[:, z:z + 128 * b], T.SR[:, 0:128 * b], s, None, A.is_ge, ev=ev)
-        ts(T.CM[:, z + 128 * b:z + 512], T.SR[:, 128 * b:512], s, None, A.is_gt, ev=ev)
+            ts(T.CM[:, z:z + 128 * b], T.SR[:, 0:128 * b], s, None, A.is_ge)
+        ts(T.CM[:, z + 128 * b:z + 512], T.SR[:, 128 * b:512], s, None, A.is_gt)
 
     def equal(b):
-        ev = "cm%d" % b if b < 3 else None
-        ts(T.CM[:, 640 * b + 512:640 * b + 640], T.SL[:, 128 * b:128 * b + 128], T.SCO[:, b:b + 1], None, A.is_equal, ev=ev)
+        ts(T.CM[:, 640 * b + 512:640 * b + 640], T.SL[:, 128 * b:128 * b + 128], T.SCO[:, b:b + 1], None, A.is_equal)
+
+    def count(b):
+        z = 640 * b
+        vr(v.tensor_tensor_scan(T.CN[:, 320 * b:320 * b + 320], T.CM[:, z:z + 320], T.CM[:, z + 320:z + 640], -256.0, A.add, A.add))
     before(0)
     before(1)
     v.wait_ge(S.sl, 1)
     equal(0)
     equal(1)
-    for b in (2, 3):
-        before(b)
-        equal(b)
-    for b in range(3):
-        a.wait_ge(S["cm%d" % b], 3 if b else 2)
-        ar(a.activation(T.CJ[:, 640 * b:640 * b + 640], T.CM[:, 640 * b:640 * b + 640], AF.Copy, accum_out=T.CN[:, b:b + 1]), "cn")
+    before(2)
+    equal(2)
     vsync()
-    vr(v.tensor_reduce(T.CN[:, 3:4], T.CM[:, 1920:2560], AxisListType.X, A.add))
+    before(3)
+    equal(3)
+    count(0)
+    count(1)
+    count(2)
     vsync()
-    v.wait_ge(S.cn, 3)
+    count(3)
+    vsync()
 
-    ts(T.OFF[:, 0:4], T.CN[:], 0.0, None, A.add)
-    ts(T.OFF[:, 4:8], T.CN[:], 528.0, None, A.add)
+    rk = T.CN[:, 319:1280:320]
+    ts(T.OFF[:, 0:4], rk, 256.0, None, A.add)
+    ts(T.OFF[:, 4:8], rk, 784.0, None, A.add)
     vsync()
+    v.wait_ge(S.zw, 3)
     vr(v.tensor_copy(T.WW[:, 0:1056].indirect(T.OFF[:, 0:8]), T.DD[:]))
     vsync()
     vr(v.transpose(T.TT[:, 0:160], T.WW[:, 0:160]))
     vr(v.transpose(T.TT[:, 160:352], T.WW[:, 512:704]))
     vsync()
     vr(v.tensor_copy(T.XX[:], T.TT[:, 0:448].indirect(T.SE[:, 0:2])), "xx")
-    for k in (2, 3):
-        ar(a.activation(T.ER[:, 512 * k:512 * k + 512], T.GR[:, 512 * k:512 * k + 512], AF.Copy), "er0")
     vsync()
     a.wait_ge(S.xx, 1)
     vr(v.tensor_copy(T.ZZ[:, 0:80:4], T.XX[:, 0:20]))
@@ -241,42 +263,51 @@ def rank_program(g, core, T, topo):
     vsync()
     num = T.SC[:, 7:80:8]
     for k in (2, 3, 0, 1):
-        ts(T.LT[:, 10 * k:10 * k + 10], num, 4.0, float(k), A.mult, A.add, ev="lt" if k > 1 else None)
-    lo = LS * r
-    vr(v.tensor_copy(T.LIN[:, lo:lo + 16], T.SC[:].indirect(T.SE[:, 2:3])), "lst")
-    vsync()
-    ts(T.LIN[:, lo + 12:lo + 22], num, 0.0, None, A.add, ev="lst")
-    ts(T.LIN[:, lo + 22:lo + 24], T.SC[:, 7:23:8], 0.0, None, A.add, ev="lst")
+        ts(T.LT[:, L * k:L * k + L], num, 4.0, float(k), A.mult, A.add, ev="lt" if k > 1 else None)
+    plain = lambda s: T.LIN[:, 16 * s:16 * s + L]
+    ts(plain(r), num, 0.0, None, A.add, ev="lst")
 
     a.wait_ge(S.lt, 2)
     for k in (2, 3):
-        ar(a.activation(T.CG[:, k:4 * K:4], T.GR[:].indirect(T.LT[:, 10 * k:10 * k + 10]), AF.Copy), "ga")
+        ar(a.activation(T.CG[:, k:4 * K:4], T.GR[:].indirect(T.LT[:, L * k:L * k + L]), AF.Copy), "ga")
+    vsync()
     for k in (0, 1):
-        vr(v.tensor_copy(T.CG[:, k:4 * K:4], T.GR[:].indirect(T.LT[:, 10 * k:10 * k + 10])))
+        vr(v.tensor_copy(T.CG[:, k:4 * K:4], T.GR[:].indirect(T.LT[:, L * k:L * k + L])))
     vsync()
     v.wait_ge(S.ga, 2)
     own = slice(K * r, K * r + K)
     vr(v.quantize_mx(T.RC[:, own], T.RP[:, own], T.CG[:]), "qc")
 
-    others = [T.cores[s] for s in order[1:]]
-    mask = topo.mask(core, others[0])
-    ne = len(topo.engines(core, others[0]))
-    ids = [DstId(rid=topo.addr(d)[0], pnc=topo.addr(d)[1]) for d in others]
+    others, roads = plan(T, topo, r)
+    off, ne = topo.mask(core, others[0]), len(topo.engines(core, others[0]))
+    hs = [c for c, _ in roads[1:]]
+    on = topo.mask(core, hs[0]) & ~off if hs else 0
+    n_on = len(topo.engines(core, hs[0])) - ne if hs else 0
+    direct = roads[0][1]
+    sent = [0]
 
-    def send(src, sem):
-        g.remote_dma_fused([RemoteDMATransfer(dst_ids=ids, dma_engine_mask=mask, remote_sem=S[sem], srcs=[src], dsts=[src] * len(ids))],
-                           local_sem=S.sent)
-    g.wait_ge(S.lst, 3)
-    send(T.LIN[:, lo:lo + LS], "li%d" % r)
+    def send(trs, n):
+        g.remote_dma_fused(trs, local_sem=S.sent)
+        sent[0] += n
+
+    def out(src, sem, hsem):
+        trs = []
+        if hs:
+            trs.append(transfer(topo, src, hs, on, S[hsem]))
+        if direct:
+            trs.append(transfer(topo, src, direct, off, S[sem]))
+        send(trs, (n_on if hs else 0) + (ne if direct else 0))
+    g.wait_ge(S.lst, 1)
+    send([transfer(topo, plain(r), others, off, S["li%d" % r])], ne)
     g.wait_ge(S.qc, 1)
-    send(T.RC[:, own].bitcast(dt.uint8), "ar%d" % r)
-    send(T.RP[:, own], "ar%d" % r)
+    out(T.RP[:, own], "ar%d" % r, "hp")
+    out(T.RC[:, own].bitcast(dt.uint8), "ar%d" % r, "hc")
 
     def decode(n):
         s = order[n]
         if n == 0:
             t.wait_ge(S.qc, 1)
-            t.wait_ge(S.on, 5)
+            t.wait_ge(S.eq, 4)
             t.wait_ge(S.sr, 2)
         else:
             t.wait_ge(S["ar%d" % s], 2 * ne)
@@ -298,20 +329,8 @@ def rank_program(g, core, T, topo):
     for n in range(N):
         decode(n)
 
-    v.wait_ge(S.mm0, 4)
-    for b in range(4):
-        tt(T.DF[:, K * b:K * b + K], T.CG[:, b:4 * K:4], T.PS[:, 512 * b:512 * b + K], A.subtract, ev="df")
-    vsync()
-    v.wait_ge(S.er0, 4)
-    vr(v.tensor_copy(T.ER[:].indirect(T.LT[:, 0:40]), T.DF[:]), "erx")
-    sy.wait_ge(S.erx, 1)
-    sy.dma_start(T.er[:], T.ER[:]).then_inc(S.st, 16)
-
-    plain = lambda s: T.LIN[:, LS * s + 12:LS * s + 22]
-    a.wait_ge(S.lst, 3)
+    a.wait_ge(S.lst, 1)
     ar(a.activation(T.SO[:], T.SR[:].indirect(plain(r)), AF.Copy), "so")
-    sy.wait_ge(S.so, 1)
-    sy.dma_start(T.sc[:], T.SO[0:1, :]).then_inc(S.st, 16)
     a.wait_ge(S.df, 4)
     unload(0)
     a.wait_ge(S.io6, 1)
@@ -319,50 +338,104 @@ def rank_program(g, core, T, topo):
         if s != r:
             a.wait_ge(S["li%d" % s], ne)
         ar(a.activation(T.NB[:, K * s:K * s + K], T.IO[:].indirect(plain(s)), AF.Copy), "nb")
-    sy.wait_ge(S.nb, N)
-    sy.dma_start(T.nb[:], T.NB[0:1, :]).then_inc(S.st, 16)
     for n in range(1, N):
         unload(n)
 
+    ts(cf(9), cf(2), cf(4)[:, 0:1] if False else T.CF[:, 8:9], None, A.mult)
+    tt(cf(10), cf(6), cf(4), A.subtract)
+    ts(cf(16), cf(0), 16.0, None, A.mult)
+    if r:
+        ts(cf(20), cf(2), 48.0, None, A.mult)
+        ts(cf(21), cf(4), 16.0, None, A.mult)
+        vsync()
+        ts(cf(22), cf(9), 64.0, None, A.mult)
+        ts(cf(24), cf(10), 0.0, 9.0, A.max, A.min)
+        tt(cf(30), cf(20), cf(21), A.add)
+        vsync()
+        tt(cf(31), cf(16), cf(22), A.subtract)
+        ts(T.SE[:, 2:4], cf(24), 8.0, 7.0, A.mult, A.add)
+        vsync()
+        tt(T.SE[:, 6:8], cf(30), cf(31), A.add)
+        vr(v.tensor_copy(T.SH[:], T.SC[:].indirect(T.SE[:, 2:3])))
+    else:
+        ts(cf(17), cf(2), 544.0, None, A.mult)
+        ts(cf(18), cf(4), 512.0, None, A.mult)
+        ts(cf(23), cf(5), 2.0, None, A.mult)
+        vsync()
+        ts(cf(19), cf(9), 1056.0, None, A.mult)
+        tt(cf(25), cf(23), cf(16), A.add)
+        tt(cf(26), cf(17), cf(18), A.add)
+        vsync()
+        tt(cf(27), cf(25), cf(26), A.add)
+        vsync()
+        tt(T.SE[:, 4:6], cf(27), cf(19), A.subtract)
+
+    v.wait_ge(S.mm0, 4)
+    for b in range(4):
+        tt(T.DF[:, K * b:K * b + K], T.CG[:, b:4 * K:4], T.PS[:, 512 * b:512 * b + K], A.subtract, ev="df")
+    vsync()
+    v.wait_ge(S.er0, 4)
+    vr(v.tensor_copy(T.ER[:].indirect(T.LT[:, 0:40]), T.DF[:]), "erx")
+
     v.wait_ge(S.io5, 1)
-    for s in range(N):
+    v.wait_ge(S.zl, 6)
+    for s in range(r if r else N):
         if s != r:
             v.wait_ge(S["li%d" % s], ne)
-        if s:
-            vr(v.tensor_copy(T.PR[:], T.LR[:, 16:528].indirect(T.LIN[:, LS * s:LS * s + 12])))
-            vsync()
         vr(v.tensor_copy(T.LR[:, 16:528].indirect(plain(s)), T.KC[:, K * s:K * s + K]))
-        if s:
-            vr(v.transpose(T.T2[:, 0:192], T.PR[:]))
         vsync()
-        if s:
-            vr(v.tensor_copy(T.PL[:, 16 * s:16 * s + 16], T.T2[:].indirect(T.SE[:, 6:7])))
-    vr(v.transpose(T.TL[:, 0:512], T.LR[:, 16:528]))
-    vr(v.transpose(T.TL[:, 512:1056], T.LR[:, 0:544]))
+    pl = lambda s: T.PL[:, 16 * s:16 * s + L]
+    if r:
+        vr(v.tensor_copy(T.PR[:], T.LR[:, 16:528].indirect(T.SH[:, 0:12])))
+        vsync()
+        vr(v.transpose(T.T2[:, 0:192], T.PR[:]))
+        vsync()
+        vr(v.tensor_copy(T.PL[:, 16 * r:16 * r + 16], T.T2[:].indirect(T.SE[:, 6:7])), "pls")
+        g.wait_ge(S.pls, 1)
+        send([transfer(topo, pl(r), others, off, S["pl%d" % r])], ne)
+    else:
+        vr(v.transpose(T.TL[:, 0:512], T.LR[:, 16:528]))
+        vr(v.transpose(T.TL[:, 512:1056], T.LR[:, 0:544]))
+        vsync()
+        vr(v.tensor_copy(T.LL[:], T.TL[:].indirect(T.SE[:, 4:6])), "pls")
+        g.wait_ge(S.pls, 1)
+        send([transfer(topo, T.LL[:], others, off, S.ll)], ne)
     vsync()
-    vr(v.tensor_copy(T.LL[:], T.TL[:].indirect(T.SE[:, 4:6])), "ll")
 
     for s in range(1, N):
+        if s != r:
+            v.wait_ge(S["pl%d" % s], ne)
         for k in ([0, 1] if s == 1 else [s]):
             v.wait_ge(S["vc%d" % turn[k]], 4)
         for b in range(4):
             o = W * b + 8 + K * s
-            tt(T.Y[:, o:o + K], T.Y[:, W * b:o].indirect(T.PL[:, 16 * s:16 * s + 10]), T.Y[:, o:o + K], A.add,
-               ev="add" if s == N - 1 else None)
+            tt(T.Y[:, o:o + K], T.Y[:, W * b:o].indirect(pl(s)), T.Y[:, o:o + K], A.add, ev="add" if s == N - 1 else None)
         vsync()
     a.wait_ge(S.add, 4)
-    a.wait_ge(S.ll, 1)
-    for h in range(2):
+    for q in (v, a):
+        if r:
+            q.wait_ge(S.ll, ne)
+        else:
+            q.wait_ge(S.pls, 1)
+    for h in range(4):
         for b in range(4):
-            out = T.AC[:, 1024 * h + b:1024 * h + 1024:4]
-            win = T.Y[:, W * b:W * b + W].indirect(T.LL[:, 16 * h:16 * h + 16])
+            dst = T.AC[:, 512 * h + b:512 * h + 512:4]
+            win = T.Y[:, W * b:W * b + W].indirect(T.LL[:, 8 * h:8 * h + 8])
             if b < 2:
-                vr(v.tensor_copy(out, win), "fv%d" % h)
+                vr(v.tensor_copy(dst, win), "fv%d" % h)
             else:
-                ar(a.activation(out, win, AF.Copy), "fa%d" % h)
+                ar(a.activation(dst, win, AF.Copy), "fa%d" % h)
+    vsync()
+
+    sy.wait_ge(S.so, 1)
+    sy.dma_start(T.sc[:], T.SO[0:1, :]).then_inc(S.st, 16)
+    sy.wait_ge(S.erx, 1)
+    sy.dma_start(T.er[:], T.ER[:]).then_inc(S.st, 16)
+    sy.wait_ge(S.nb, N)
+    sy.dma_start(T.nb[:], T.NB[0:1, :]).then_inc(S.st, 16)
+    for h in range(4):
         sy.wait_ge(S["fv%d" % h], 2)
         sy.wait_ge(S["fa%d" % h], 2)
-        sy.dma_start(T.acc[:, 1024 * h:1024 * h + 1024], T.AC[:, 1024 * h:1024 * h + 1024]).then_inc(S.st, 16)
-    vsync()
-    g.wait_ge(S.sent, 3 * ne)
-    sy.wait_ge(S.st, 80)
+        sy.dma_start(T.acc[:, 512 * h:512 * h + 512], T.AC[:, 512 * h:512 * h + 512]).then_inc(S.st, 16)
+    g.wait_ge(S.sent, sent[0])
+    sy.wait_ge(S.st, 16 * 7)

@@ -4,7 +4,7 @@ from concourse.mybir import dt, AluOpType, ActivationFunctionType
 N, TC, K = 6, 512, 160
 W = 8 + N * K
 L = K // 16
-SHARE = [(2, 2, 1)] * N
+SHARE = [(3, 1, 1)] + [(2, 2, 1)] * (N - 1)
 
 F, B, I, U, C8, P8 = "float32", "bfloat16", "int32", "uint16", "float8_e4m3fn_x4", "uint8"
 SCRATCH = {
@@ -14,26 +14,29 @@ SCRATCH = {
     "ON": ("sbuf", [128, 640], B), "MM": ("sbuf", [128, 516], B),
     "EQ": ("sbuf", [128, 512], C8), "EP": ("sbuf", [128, 512], P8),
     "PS": ("psum", [128, 4096], F),
-    "SR": ("sbuf", [128, 512], F), "SL": ("sbuf", [128, 512], F), "SCO": ("sbuf", [128, 4], F),
-    "CM": ("sbuf", [128, 2560], B), "CN": ("sbuf", [128, 1280], B),
+    "SR": ("sbuf", [128, 512], F), "SL": ("sbuf", [128, 512], F), "SCO": ("sbuf", [128, 4], F), "SN": ("sbuf", [128, 4], F),
+    "SG": ("sbuf", [128, 1024], B), "CM": ("sbuf", [128, 2560], B), "CN": ("sbuf", [128, 1280], B),
     "OFF": ("sbuf", [128, 8], U), "DD": ("sbuf", [128, 128], F), "WW": ("sbuf", [128, 1056], F),
     "TT": ("sbuf", [128, 448], F), "XX": ("sbuf", [128, 32], F), "ZZ": ("sbuf", [128, 80], F),
-    "RM": ("sbuf", [128, 80], F), "SC": ("sbuf", [128, 80], F),
-    "LT": ("sbuf", [128, 40], U), "LIN": ("sbuf", [128, 16 * N], U), "SH": ("sbuf", [128, 16], U),
+    "RM": ("sbuf", [128, 80], F), "SC": ("sbuf", [128, 80], F), "S2": ("sbuf", [128, 80], F),
+    "LT": ("sbuf", [128, 40], U), "LP": ("sbuf", [128, 16], U),
+    "QM": ("sbuf", [128, 4], F), "QX": ("sbuf", [128, 4], F), "QS": ("sbuf", [128, 4], F),
+    "RK": ("sbuf", [128, 8 * N], U), "QV": ("sbuf", [128, 4 * N], F), "RN": ("sbuf", [128, 4 * N], F), "PX": ("sbuf", [128, 4 * N], F),
+    "ZT": ("sbuf", [128, 32], F), "EX": ("sbuf", [128, 128], F), "ET": ("sbuf", [128, 128], F), "D2": ("sbuf", [128, 128], F),
+    "LQ": ("sbuf", [128, 64], F), "LA": ("sbuf", [128, 32], F), "LB": ("sbuf", [128, 32], F),
     "CG": ("sbuf", [128, 4 * K], B), "RC": ("sbuf", [128, N * K], C8), "RP": ("sbuf", [128, N * K], P8),
-    "DF": ("sbuf", [128, 4 * K], F), "ER": ("sbuf", [128, 2048], F), "Y": ("sbuf", [128, 4 * W], F),
-    "LR": ("sbuf", [128, 544], F), "KC": ("sbuf", [128, N * K], F), "PR": ("sbuf", [128, 192], F),
-    "T2": ("sbuf", [128, 288], F), "PL": ("sbuf", [128, 16 * N], U), "TL": ("sbuf", [128, 1056], F),
-    "LL": ("sbuf", [128, 32], U), "AC": ("sbuf", [128, 2048], F), "IO": ("sbuf", [128, 512], F),
-    "NB": ("sbuf", [128, N * K], F), "SO": ("sbuf", [128, K], F),
+    "DF": ("sbuf", [128, 4 * K], F), "ER": ("sbuf", [128, 2048], F), "Y": ("sbuf", [128, 4 * W], F), "TM": ("sbuf", [128, 2 * K], F),
+    "PL": ("sbuf", [128, 16 * N], U), "LL": ("sbuf", [128, 32], U), "AC": ("sbuf", [128, 2048], F), "IO": ("sbuf", [128, 512], F),
+    "NB": ("sbuf", [128, 256], F), "ND": ("dram", [N, 128, 2], F), "SO": ("sbuf", [128, K], F),
     "VI": ("sbuf", [128, 32], I), "VJ": ("sbuf", [128, 32], I), "UL": ("sbuf", [128, 32], U),
-    "V2": ("sbuf", [128, 2], I), "CI": ("sbuf", [128, 16], I), "CF": ("sbuf", [128, 64], F),
-    "SE": ("sbuf", [128, 8], U), "D0": ("sbuf", [128, 128], F), "R0": ("sbuf", [128, 80], F),
+    "V2": ("sbuf", [128, 2], I), "CI": ("sbuf", [128, 18], I), "CF": ("sbuf", [128, 64], F),
+    "SE": ("sbuf", [128, 4], U), "SD": ("sbuf", [128, 8], U), "D0": ("sbuf", [128, 128], F), "R0": ("sbuf", [128, 80], F),
+    "R1": ("sbuf", [128, 24], F), "D8": ("sbuf", [128, 8], F),
 }
-_EV = ["v", "a", "t", "ld_u", "ld_g0", "ld_g1", "on", "ul", "io1", "io2", "io3", "io4", "io5", "io6", "mst", "ut", "uq",
-       "gq0", "gq1", "ms0", "ms1", "sr", "sco", "sl", "er0", "xx", "za", "lt", "zw", "zl", "eq",
-       "ga", "lst", "qc", "df", "erx", "so", "nb", "add", "ll", "st", "sent", "pls", "hp", "hc"]
-SEMAPHORES = _EV + ["%s%d" % (e, n) for e in ("mm", "vc", "li", "ar", "pl") for n in range(N)] \
+_EV = ["v", "a", "t", "ld_u", "ld_g0", "ld_g1", "on", "ul", "io1", "io2", "io3", "io4", "io5", "io6", "io7", "mst", "ut", "uq",
+       "gq0", "gq1", "ms0", "ms1", "sr", "sco", "sg", "sl", "er0", "xx", "za", "lt", "zw", "zl", "eq", "rks", "px", "lq",
+       "ga", "lst", "qc", "df", "erx", "so", "nb", "nd", "ll", "st", "sent", "pls", "hp", "hc", "tm", "c0", "c1", "c2", "c3"]
+SEMAPHORES = _EV + ["%s%d" % (e, n) for e in ("mm", "vc", "li", "rk", "ar", "pl") for n in range(N)] \
     + ["%s%d" % (e, n) for e in ("fv", "fa") for n in range(4)]
 
 
@@ -50,12 +53,13 @@ def tracked(q, T, name):
         for e in list(pend):
             q.wait_ge(T.sem[e], pend[e])
         pend.clear()
+        return dict(tot)
     return rec, sync
 
 
 def plan(T, topo, r):
     core = T.cores[r]
-    others = [T.cores[(r + d) % N] for d in range(1, N)]
+    others = [T.cores[(r - d) % N] for d in range(1, N)]
     hs = [c for c in topo.cores_of(core) if c != core and all(topo.may_write(c, d) for d in others)]
     hs.sort(key=lambda c: topo.die(c) == topo.die(core))
     out, i = [], 0
@@ -66,12 +70,9 @@ def plan(T, topo, r):
     return others, out
 
 
-def ids_of(topo, cores):
-    return [DstId(rid=topo.addr(d)[0], pnc=topo.addr(d)[1]) for d in cores]
-
-
 def transfer(topo, src, cores, mask, sem):
-    return RemoteDMATransfer(dst_ids=ids_of(topo, cores), dma_engine_mask=mask, remote_sem=sem, srcs=[src], dsts=[src] * len(cores))
+    ids = [DstId(rid=topo.addr(d)[0], pnc=topo.addr(d)[1]) for d in cores]
+    return RemoteDMATransfer(dst_ids=ids, dma_engine_mask=mask, remote_sem=sem, srcs=[src], dsts=[src] * len(cores))
 
 
 def helper_program(g, core, T, topo):
@@ -112,25 +113,31 @@ def rank_program(g, core, T, topo):
     def tt(out, x, y, op, ev=None):
         vr(v.tensor_tensor(out, x, y, op), ev)
 
+    def iota(out, pattern, base, ev):
+        g.iota(out, pattern, base, 0, allow_small_or_imprecise_dtypes=True).then_inc(S[ev], 1)
+
     sy.dma_start(T.U4[:, 0:4], T.u[:, 0:4]).then_inc(S.ld_u, 16)
     sy.dma_start(T.GR[:, 0:1024], T.gr[:, 0:1024]).then_inc(S.ld_g0, 16)
     a.dma_start(T.GR[:, 1024:2048], T.gr[:, 1024:2048]).then_inc(S.ld_g1, 16)
 
     g.iota(T.VI[:], [[0, 32]], 0, 1).then_inc(S.io1, 1)
     g.iota(T.V2[:], [[128, 2]], 0, 1).then_inc(S.io2, 1)
-    g.iota(T.D0[:], [[0, 2], [128, 4], [1, 16]], 0, 0, allow_small_or_imprecise_dtypes=True).then_inc(S.io3, 1)
-    g.iota(T.R0[:], [[0, 10], [1, 8]], 0, 0, allow_small_or_imprecise_dtypes=True).then_inc(S.io4, 1)
+    iota(T.D0[:], [[0, 2], [128, 4], [1, 16]], 0, "io3")
+    iota(T.R0[:], [[0, 10], [1, 8]], 0, "io4")
     g.wait_ge(S.on, 1)
     g.affine_select(T.MM[:], T.ON[:, 0:516], [[-1, 516]], A.is_equal, 0.0, 3, 4).then_inc(S.mst, 1)
+    iota(T.R1[:], [[0, 4], [1, N]], 0, "io5")
+    iota(T.D8[:], [[0, 2], [32, 4]], 0, "io7")
     g.wait_ge(S.sr, 2)
     g.affine_select(T.SL[:], T.SR[:], [[0, 4], [-1, 128]], A.is_gt, -1.0, 0, 1).then_inc(S.sl, 1)
-    g.iota(T.KC[:], [[1, N * K]], 8, 0, allow_small_or_imprecise_dtypes=True).then_inc(S.io5, 1)
-    g.iota(T.IO[:], [[1, 512]], 0, 0, allow_small_or_imprecise_dtypes=True).then_inc(S.io6, 1)
+    iota(T.IO[:], [[1, 512]], 0, "io6")
 
     a.wait_ge(S.on, 1)
     for out, n, ev in ((T.WW[:, 0:160], 160, "zw"), (T.WW[:, 512:704], 192, "zw"), (T.TT[:, 352:448], 96, "zw"),
-                       (T.T2[:, 192:288], 96, "zl"), (T.LR[:], 544, "zl")):
+                       (T.ZT[:], 32, "zl"), (T.LQ[:, 16:32], 16, "zl")):
         ar(a.activation(out, T.ON[:, 0:n], AF.Copy, scale=0.0), ev)
+    for b in range(4):
+        ar(a.activation(T.Y[:, W * b:W * b + 8], T.ON[:, 0:8], AF.Copy, scale=0.0), "zl")
     a.wait_ge(S.ld_u, 16)
     a.wait_ge(S.ul, 1)
     ar(a.activation(T.UT[:], T.U4[:, 0:4].indirect(T.UL[:, 0:32]), AF.Copy), "ut")
@@ -149,10 +156,10 @@ def rank_program(g, core, T, topo):
     ts(ci(3), T.V2[:], 1, 1, A.arith_shift_right, A.bitwise_and)
     ts(ci(4), T.V2[:], 4, 1, A.arith_shift_right, A.bitwise_and)
     ts(ci(5), T.V2[:], 128, None, A.bitwise_and)
-    ts(ci(6), T.V2[:], 15, None, A.bitwise_and)
+    ts(ci(6), T.V2[:], 31, None, A.bitwise_and)
     ts(ci(7), T.V2[:], 112, None, A.bitwise_and)
     vsync()
-    vr(v.tensor_copy(T.CF[:, 0:16], T.CI[:]))
+    vr(v.tensor_copy(T.CF[:, 0:16], T.CI[:, 0:16]))
     vsync()
     tt(cf(8), cf(3), cf(4), A.mult)
     ts(cf(11), cf(1), 8.0, None, A.mult)
@@ -195,8 +202,11 @@ def rank_program(g, core, T, topo):
         ar(a.activation(T.SR[:, 256 * h:256 * h + 256], T.PS[:, 512 * h:512 * h + 256], AF.Abs), "sr")
     a.wait_ge(S.t, 4)
     ar(a.activation(T.SCO[:], T.PS[:, 2048:4096:512], AF.Abs), "sco")
-    for b in range(4):
-        ar(a.activation(T.Y[:, W * b:W * b + 8], T.ON[:, 0:8], AF.Copy, scale=0.0), "zl")
+    async_()
+    ar(a.activation(T.SN[:], T.SCO[:], AF.Copy, scale=-1.0))
+    async_()
+    for b in (2, 3):
+        ar(a.activation(T.SG[:, 512 * b - 1024:512 * b - 512], T.SR[:], AF.Sign, bias=T.SN[:, b:b + 1]), "sg")
     for k in range(4):
         ar(a.activation(T.ER[:, 512 * k:512 * k + 512], T.GR[:, 512 * k:512 * k + 512], AF.Copy), "er0")
 
@@ -205,10 +215,10 @@ def rank_program(g, core, T, topo):
 
     def before(b):
         z = 640 * b
-        s = T.SCO[:, b:b + 1]
+        s, x = (T.SCO[:, b:b + 1], lambda i, j: T.SR[:, i:j]) if b < 2 else (0.0, lambda i, j: T.SG[:, 512 * b - 1024 + i:512 * b - 1024 + j])
         if b:
-            ts(T.CM[:, z:z + 128 * b], T.SR[:, 0:128 * b], s, None, A.is_ge)
-        ts(T.CM[:, z + 128 * b:z + 512], T.SR[:, 128 * b:512], s, None, A.is_gt)
+            ts(T.CM[:, z:z + 128 * b], x(0, 128 * b), s, None, A.is_ge)
+        ts(T.CM[:, z + 128 * b:z + 512], x(128 * b, 512), s, None, A.is_gt)
 
     def equal(b):
         ts(T.CM[:, 640 * b + 512:640 * b + 640], T.SL[:, 128 * b:128 * b + 128], T.SCO[:, b:b + 1], None, A.is_equal)
@@ -219,53 +229,57 @@ def rank_program(g, core, T, topo):
     before(0)
     before(1)
     v.wait_ge(S.sl, 1)
-    equal(0)
-    equal(1)
+    for b in range(4):
+        equal(b)
+    v.wait_ge(S.sg, 2)
     before(2)
-    equal(2)
     vsync()
     before(3)
-    equal(3)
-    count(0)
-    count(1)
-    count(2)
+    for b in range(3):
+        count(b)
     vsync()
     count(3)
     vsync()
 
+    def permute(val, out, between=None):
+        vr(v.tensor_copy(T.WW[:, 0:1056].indirect(T.OFF[:, 0:8]), val))
+        vsync()
+        if between:
+            between()
+        vr(v.transpose(T.TT[:, 0:160], T.WW[:, 0:160]))
+        vr(v.transpose(T.TT[:, 160:352], T.WW[:, 512:704]))
+        vsync()
+        vr(v.tensor_copy(T.XX[:], T.TT[:, 0:448].indirect(T.SE[:, 0:2])), "xx")
+        n = vsync()["xx"]
+        a.wait_ge(S.xx, n)
+        vr(v.tensor_copy(T.ZZ[:, 0:80:4], T.XX[:, 0:20]))
+        for p in (0, 64):
+            vr(v.tensor_copy(T.ZZ[64 - p:128 - p, 2:80:4], T.XX[p:p + 64, 0:20]))
+        for d in (1, 3):
+            for p in range(4):
+                o = 32 * (p ^ d)
+                dst, src = T.ZZ[o:o + 32, d:80:4], T.XX[32 * p:32 * p + 32, 0:20]
+                if d == 1 and p < 3:
+                    vr(v.tensor_copy(dst, src))
+                else:
+                    ar(a.activation(dst, src, AF.Copy), "za")
+        vsync()
+        v.wait_ge(S.za, 5 * n)
+        vr(v.tensor_tensor_scan(out[:], T.RM[:], T.ZZ[:], 0.0, A.mult, A.add))
+        vsync()
+        return out[:, 7:80:8]
+
     rk = T.CN[:, 319:1280:320]
     ts(T.OFF[:, 0:4], rk, 256.0, None, A.add)
     ts(T.OFF[:, 4:8], rk, 784.0, None, A.add)
+    ts(T.QM[:], rk, -96.0, None, A.is_lt)
+    ts(T.QX[:], rk, float(264 + K * r), None, A.add)
     vsync()
     v.wait_ge(S.zw, 3)
-    vr(v.tensor_copy(T.WW[:, 0:1056].indirect(T.OFF[:, 0:8]), T.DD[:]))
-    vsync()
-    vr(v.transpose(T.TT[:, 0:160], T.WW[:, 0:160]))
-    vr(v.transpose(T.TT[:, 160:352], T.WW[:, 512:704]))
-    vsync()
-    vr(v.tensor_copy(T.XX[:], T.TT[:, 0:448].indirect(T.SE[:, 0:2])), "xx")
-    vsync()
-    a.wait_ge(S.xx, 1)
-    vr(v.tensor_copy(T.ZZ[:, 0:80:4], T.XX[:, 0:20]))
-    for p in (0, 64):
-        vr(v.tensor_copy(T.ZZ[64 - p:128 - p, 2:80:4], T.XX[p:p + 64, 0:20]))
-    for d in (1, 3):
-        for p in range(4):
-            o = 32 * (p ^ d)
-            dst, src = T.ZZ[o:o + 32, d:80:4], T.XX[32 * p:32 * p + 32, 0:20]
-            if d == 1 and p < 3:
-                vr(v.tensor_copy(dst, src))
-            else:
-                ar(a.activation(dst, src, AF.Copy), "za")
-    vsync()
-    v.wait_ge(S.za, 5)
-    vr(v.tensor_tensor_scan(T.SC[:], T.RM[:], T.ZZ[:], 0.0, A.mult, A.add))
-    vsync()
-    num = T.SC[:, 7:80:8]
+    tt(T.QS[:], T.QM[:], T.QX[:], A.mult)
+    num = permute(T.DD[:], T.SC, lambda: ts(T.RK[:, 8 * r:8 * r + 4], T.QS[:], 0.0, None, A.add, ev="rks"))
     for k in (2, 3, 0, 1):
         ts(T.LT[:, L * k:L * k + L], num, 4.0, float(k), A.mult, A.add, ev="lt" if k > 1 else None)
-    plain = lambda s: T.LIN[:, 16 * s:16 * s + L]
-    ts(plain(r), num, 0.0, None, A.add, ev="lst")
 
     a.wait_ge(S.lt, 2)
     for k in (2, 3):
@@ -277,6 +291,8 @@ def rank_program(g, core, T, topo):
     v.wait_ge(S.ga, 2)
     own = slice(K * r, K * r + K)
     vr(v.quantize_mx(T.RC[:, own], T.RP[:, own], T.CG[:]), "qc")
+    ts(T.LP[:, 0:L], num, 0.0, None, A.add, ev="lst")
+    ts(T.LP[:, L:16], T.SC[:, 7:55:8], 0.0, None, A.add, ev="lst")
 
     others, roads = plan(T, topo, r)
     off, ne = topo.mask(core, others[0]), len(topo.engines(core, others[0]))
@@ -297,11 +313,18 @@ def rank_program(g, core, T, topo):
         if direct:
             trs.append(transfer(topo, src, direct, off, S[sem]))
         send(trs, (n_on if hs else 0) + (ne if direct else 0))
-    g.wait_ge(S.lst, 1)
-    send([transfer(topo, plain(r), others, off, S["li%d" % r])], ne)
+    g.wait_ge(S.rks, 1)
+    send([transfer(topo, T.RK[:, 8 * r:8 * r + 4], others, off, S["rk%d" % r])], ne)
     g.wait_ge(S.qc, 1)
     out(T.RP[:, own], "ar%d" % r, "hp")
     out(T.RC[:, own].bitcast(dt.uint8), "ar%d" % r, "hc")
+
+    mixed = lambda s: s not in (0, r)
+
+    def free(n):
+        t.wait_ge(S["vc%d" % n], 3 if mixed(order[n]) else 4)
+        if mixed(order[n]):
+            t.wait_ge(S.c3, order[n])
 
     def decode(n):
         s = order[n]
@@ -314,7 +337,7 @@ def rank_program(g, core, T, topo):
             if n == 1:
                 t.wait_ge(S.sco, 1)
             else:
-                t.wait_ge(S["vc%d" % (n - 2)], 4)
+                free(n - 2)
         z = 2048 * (n % 2)
         for b in range(4):
             t.matmul_mx(T.PS[:, z + 512 * b:z + 512 * b + K], T.EQ[:, 128 * b:128 * b + 128], T.EP[:, 128 * b:128 * b + 128],
@@ -323,119 +346,147 @@ def rank_program(g, core, T, topo):
     def unload(n):
         s, z = order[n], 2048 * (n % 2)
         a.wait_ge(S["mm%d" % n], 4)
-        for b in range(4):
+        for b in range(3 if mixed(s) else 4):
             o = W * b + 8 + K * s
             ar(a.activation(T.Y[:, o:o + K], T.PS[:, z + 512 * b:z + 512 * b + K], AF.Copy), "vc%d" % n)
     for n in range(N):
         decode(n)
 
-    a.wait_ge(S.lst, 1)
-    ar(a.activation(T.SO[:], T.SR[:].indirect(plain(r)), AF.Copy), "so")
-    a.wait_ge(S.df, 4)
-    unload(0)
     a.wait_ge(S.io6, 1)
-    for s in order:
-        if s != r:
-            a.wait_ge(S["li%d" % s], ne)
-        ar(a.activation(T.NB[:, K * s:K * s + K], T.IO[:].indirect(plain(s)), AF.Copy), "nb")
-    for n in range(1, N):
-        unload(n)
+    a.wait_ge(S.lst, 2)
+    ar(a.activation(T.NB[:], T.IO[:].indirect(T.LP[:]), AF.Copy), "nb")
+    ar(a.activation(T.SO[:], T.SR[:].indirect(T.LP[:, 0:L]), AF.Copy), "so")
 
-    ts(cf(9), cf(2), cf(4)[:, 0:1] if False else T.CF[:, 8:9], None, A.mult)
-    tt(cf(10), cf(6), cf(4), A.subtract)
-    ts(cf(16), cf(0), 16.0, None, A.mult)
-    if r:
-        ts(cf(20), cf(2), 48.0, None, A.mult)
-        ts(cf(21), cf(4), 16.0, None, A.mult)
-        vsync()
-        ts(cf(22), cf(9), 64.0, None, A.mult)
-        ts(cf(24), cf(10), 0.0, 9.0, A.max, A.min)
-        tt(cf(30), cf(20), cf(21), A.add)
-        vsync()
-        tt(cf(31), cf(16), cf(22), A.subtract)
-        ts(T.SE[:, 2:4], cf(24), 8.0, 7.0, A.mult, A.add)
-        vsync()
-        tt(T.SE[:, 6:8], cf(30), cf(31), A.add)
-        vr(v.tensor_copy(T.SH[:], T.SC[:].indirect(T.SE[:, 2:3])))
-    else:
-        ts(cf(17), cf(2), 544.0, None, A.mult)
-        ts(cf(18), cf(4), 512.0, None, A.mult)
-        ts(cf(23), cf(5), 2.0, None, A.mult)
-        vsync()
-        ts(cf(19), cf(9), 1056.0, None, A.mult)
-        tt(cf(25), cf(23), cf(16), A.add)
-        tt(cf(26), cf(17), cf(18), A.add)
-        vsync()
-        tt(cf(27), cf(25), cf(26), A.add)
-        vsync()
-        tt(T.SE[:, 4:6], cf(27), cf(19), A.subtract)
+    ts(cf(9), cf(2), T.CF[:, 8:9], None, A.mult)
+    ts(cf(16), cf(0), 0.5, None, A.mult)
+    ts(cf(17), cf(5), 0.0625, None, A.mult)
+    tt(cf(18), cf(2), cf(4), A.add)
+    v.wait_ge(S.io5, 1)
+    ts(T.RN[:], T.R1[:], 1.0, None, A.min)
+    v.wait_ge(S.io7, 1)
+    ts(T.SD[:], T.D8[:], T.CF[:, 12:13], None, A.add)
+    vsync()
+    ts(cf(19), cf(9), 64.0, None, A.mult)
+    ts(cf(20), cf(18), 32.0, None, A.mult)
+    tt(cf(21), cf(16), cf(17), A.add)
+    vsync()
+    tt(cf(22), cf(20), cf(19), A.subtract)
+    vsync()
+    tt(T.SE[:, 2:4], cf(21), cf(22), A.add)
 
     v.wait_ge(S.mm0, 4)
     for b in range(4):
         tt(T.DF[:, K * b:K * b + K], T.CG[:, b:4 * K:4], T.PS[:, 512 * b:512 * b + K], A.subtract, ev="df")
+    a.wait_ge(S.df, 4)
+    unload(0)
+
+    for s in order[1:]:
+        v.wait_ge(S["rk%d" % s], ne)
+    for b in range(4):
+        vr(v.tensor_copy(T.QV[:, N * b:N * b + N], T.RK[:, b:8 * N:8]))
+    vsync()
+    vr(v.tensor_tensor_scan(T.PX[:], T.RN[:], T.QV[:], 0.0, A.mult, A.max), "px")
+    vsync()
+    v.wait_ge(S.zl, 6)
+    pl = lambda s: T.PL[:, 16 * s:16 * s + L]
+    if r:
+        for b in range(4):
+            c = N * b + r - 1
+            ts(T.EX[:, 32 * b:32 * b + 32], T.ZT[:], T.PX[:, c:c + 1], None, A.add)
+        vsync()
+        vr(v.transpose(T.ET[:], T.EX[:]))
+        vsync()
+        vr(v.tensor_copy(T.D2[:], T.ET[:].indirect(T.SD[:, 0:8])))
+        vsync()
+        ts(pl(r), permute(T.D2[:], T.S2), 0.0, None, A.add, ev="pls")
+        g.wait_ge(S.pls, 1)
+        send([transfer(topo, pl(r), others, off, S["pl%d" % r])], ne)
+    g.wait_ge(S.nd, 16)
+    send([transfer(topo, T.ND[r], others, off, S["li%d" % r])], ne)
+    a.wait_ge(S.px, 1)
+    for p in range(4):
+        for d in range(4):
+            ar(a.activation(T.LQ[32 * d:32 * d + 32, p:16:4], T.PX[32 * p:32 * p + 32, N - 1:4 * N:N], AF.Copy), "lq")
+
     vsync()
     v.wait_ge(S.er0, 4)
     vr(v.tensor_copy(T.ER[:].indirect(T.LT[:, 0:40]), T.DF[:]), "erx")
-
-    v.wait_ge(S.io5, 1)
-    v.wait_ge(S.zl, 6)
-    for s in range(r if r else N):
-        if s != r:
-            v.wait_ge(S["li%d" % s], ne)
-        vr(v.tensor_copy(T.LR[:, 16:528].indirect(plain(s)), T.KC[:, K * s:K * s + K]))
-        vsync()
-    pl = lambda s: T.PL[:, 16 * s:16 * s + L]
-    if r:
-        vr(v.tensor_copy(T.PR[:], T.LR[:, 16:528].indirect(T.SH[:, 0:12])))
-        vsync()
-        vr(v.transpose(T.T2[:, 0:192], T.PR[:]))
-        vsync()
-        vr(v.tensor_copy(T.PL[:, 16 * r:16 * r + 16], T.T2[:].indirect(T.SE[:, 6:7])), "pls")
-        g.wait_ge(S.pls, 1)
-        send([transfer(topo, pl(r), others, off, S["pl%d" % r])], ne)
-    else:
-        vr(v.transpose(T.TL[:, 0:512], T.LR[:, 16:528]))
-        vr(v.transpose(T.TL[:, 512:1056], T.LR[:, 0:544]))
-        vsync()
-        vr(v.tensor_copy(T.LL[:], T.TL[:].indirect(T.SE[:, 4:6])), "pls")
-        g.wait_ge(S.pls, 1)
-        send([transfer(topo, T.LL[:], others, off, S.ll)], ne)
+    v.wait_ge(S.lq, 16)
+    vr(v.transpose(T.LA[:], T.LQ[:, 0:32]))
+    vsync()
+    vr(v.tensor_copy(T.LB[:, 0:16], T.LA[:, 16:32]))
+    vr(v.tensor_copy(T.LB[:, 16:32], T.LA[:, 0:16]))
+    vsync()
+    vr(v.transpose(T.LQ[:, 32:64], T.LB[:]))
+    vsync()
+    vr(v.tensor_copy(T.LL[:], T.LQ[:].indirect(T.SE[:, 2:4])), "ll")
     vsync()
 
+    tm = lambda s: T.TM[:, K * (s % 2):K * (s % 2) + K]
+    for n in range(1, N):
+        s = order[n]
+        unload(n)
+        if mixed(s):
+            if s == 1 or (s == 2 and r == 1):
+                async_()
+            a.wait_ge(S["pl%d" % s], ne)
+            if s > 1:
+                a.wait_ge(S.c3, s - 1)
+            ar(a.activation(tm(s), T.Y[:, 3 * W:3 * W + 8 + K * s].indirect(pl(s)), AF.Copy), "tm")
+    nt = 0
     for s in range(1, N):
         if s != r:
             v.wait_ge(S["pl%d" % s], ne)
         for k in ([0, 1] if s == 1 else [s]):
-            v.wait_ge(S["vc%d" % turn[k]], 4)
-        for b in range(4):
+            v.wait_ge(S["vc%d" % turn[k]], 3 if mixed(k) else 4)
+        for b in (3, 0, 1, 2):
             o = W * b + 8 + K * s
-            tt(T.Y[:, o:o + K], T.Y[:, W * b:o].indirect(pl(s)), T.Y[:, o:o + K], A.add, ev="add" if s == N - 1 else None)
-        vsync()
-    a.wait_ge(S.add, 4)
-    for q in (v, a):
-        if r:
-            q.wait_ge(S.ll, ne)
-        else:
-            q.wait_ge(S.pls, 1)
-    for h in range(4):
-        for b in range(4):
-            dst = T.AC[:, 512 * h + b:512 * h + 512:4]
-            win = T.Y[:, W * b:W * b + W].indirect(T.LL[:, 8 * h:8 * h + 8])
-            if b < 2:
-                vr(v.tensor_copy(dst, win), "fv%d" % h)
+            if s > 1:
+                v.wait_ge(S["c%d" % b], s - 1)
+            if b == 3 and mixed(s):
+                nt += 1
+                v.wait_ge(S.tm, nt)
+                z = 2048 * (turn[s] % 2) + 512 * b
+                tt(T.Y[:, o:o + K], tm(s), T.PS[:, z:z + K], A.add, ev="c3")
             else:
-                ar(a.activation(dst, win, AF.Copy), "fa%d" % h)
+                tt(T.Y[:, o:o + K], T.Y[:, W * b:o].indirect(pl(s)), T.Y[:, o:o + K], A.add, ev="c%d" % b)
+
+    def lay(b, h):
+        return T.AC[:, 512 * h + b:512 * h + 512:4], T.Y[:, W * b:W * b + W].indirect(T.LL[:, 8 * h:8 * h + 8])
+
+    def lay_a(b, h):
+        dst, win = lay(b, h)
+        ar(a.activation(dst, win, AF.Copy), "fa%d" % h)
+    a.wait_ge(S.ll, 1)
+    a.wait_ge(S.c3, N - 1)
+    for h in range(4):
+        lay_a(3, h)
+    a.wait_ge(S.c2, N - 1)
+    a.wait_ge(S.c1, N - 1)
+    v.wait_ge(S.c0, N - 1)
+    for h in range(4):
+        for b in ((0, 1) if h < 2 else (0,)):
+            if h == 0 and b == 1:
+                v.wait_ge(S.c1, N - 1)
+            dst, win = lay(b, h)
+            vr(v.tensor_copy(dst, win), "fv%d" % h)
+        for b in ((2,) if h < 2 else (2, 1)):
+            lay_a(b, h)
     vsync()
 
+    sy.wait_ge(S.nb, 1)
+    sy.dma_start(T.ND[r], T.NB[0:1, :]).then_inc(S.nd, 16)
+    sy.dma_start(T.nb[r:r + 1, :], T.NB[0:1, 0:K]).then_inc(S.st, 16)
     sy.wait_ge(S.so, 1)
     sy.dma_start(T.sc[:], T.SO[0:1, :]).then_inc(S.st, 16)
     sy.wait_ge(S.erx, 1)
     sy.dma_start(T.er[:], T.ER[:]).then_inc(S.st, 16)
-    sy.wait_ge(S.nb, N)
-    sy.dma_start(T.nb[:], T.NB[0:1, :]).then_inc(S.st, 16)
+    for s in order[1:]:
+        sy.wait_ge(S["li%d" % s], ne)
+        sy.dma_start(T.nb[s:s + 1, :], T.ND[s, 0:K // 2, :]).then_inc(S.st, 16)
     for h in range(4):
-        sy.wait_ge(S["fv%d" % h], 2)
-        sy.wait_ge(S["fa%d" % h], 2)
+        sy.wait_ge(S["fv%d" % h], 2 if h < 2 else 1)
+        sy.wait_ge(S["fa%d" % h], 2 if h < 2 else 3)
         sy.dma_start(T.acc[:, 512 * h:512 * h + 512], T.AC[:, 512 * h:512 * h + 512]).then_inc(S.st, 16)
     g.wait_ge(S.sent, sent[0])
-    sy.wait_ge(S.st, 16 * 7)
+    sy.wait_ge(S.st, 16 * (N + 6))

from concourse.bass import DstId, RemoteDMATransfer
from concourse.mybir import dt, AluOpType, ActivationFunctionType

N, TC, K = 6, 512, 160
W = 8 + N * K
L = K // 16
SHARE = [(3, 1, 1)] + [(2, 2, 1)] * (N - 1)

F, B, I, U, C8, P8 = "float32", "bfloat16", "int32", "uint16", "float8_e4m3fn_x4", "uint8"
SCRATCH = {
    "U4": ("sbuf", [128, 16], B), "UT": ("sbuf", [128, 512], B),
    "UQ": ("sbuf", [128, 128], C8), "UP": ("sbuf", [128, 128], P8),
    "GR": ("sbuf", [128, 2048], B), "GQ": ("sbuf", [128, 512], C8), "GP": ("sbuf", [128, 512], P8),
    "ON": ("sbuf", [128, 640], B), "MM": ("sbuf", [128, 516], B),
    "EQ": ("sbuf", [128, 512], C8), "EP": ("sbuf", [128, 512], P8),
    "PS": ("psum", [128, 4096], F),
    "SR": ("sbuf", [128, 512], F), "SL": ("sbuf", [128, 512], F), "SCO": ("sbuf", [128, 4], F), "SN": ("sbuf", [128, 4], F),
    "SG": ("sbuf", [128, 1024], B), "CM": ("sbuf", [128, 2560], B), "CN": ("sbuf", [128, 1280], B),
    "OFF": ("sbuf", [128, 8], U), "DD": ("sbuf", [128, 128], F), "WW": ("sbuf", [128, 1056], F),
    "TT": ("sbuf", [128, 448], F), "XX": ("sbuf", [128, 32], F), "ZZ": ("sbuf", [128, 80], F),
    "RM": ("sbuf", [128, 80], F), "SC": ("sbuf", [128, 80], F), "S2": ("sbuf", [128, 80], F),
    "LT": ("sbuf", [128, 40], U), "LP": ("sbuf", [128, 16], U),
    "QM": ("sbuf", [128, 4], F), "QX": ("sbuf", [128, 4], F), "QS": ("sbuf", [128, 4], F),
    "RK": ("sbuf", [128, 8 * N], U), "QV": ("sbuf", [128, 4 * N], F), "RN": ("sbuf", [128, 4 * N], F), "PX": ("sbuf", [128, 4 * N], F),
    "ZT": ("sbuf", [128, 32], F), "EX": ("sbuf", [128, 128], F), "ET": ("sbuf", [128, 128], F), "D2": ("sbuf", [128, 128], F),
    "LQ": ("sbuf", [128, 64], F), "LA": ("sbuf", [128, 32], F), "LB": ("sbuf", [128, 32], F),
    "CG": ("sbuf", [128, 4 * K], B), "RC": ("sbuf", [128, N * K], C8), "RP": ("sbuf", [128, N * K], P8),
    "DF": ("sbuf", [128, 4 * K], F), "ER": ("sbuf", [128, 2048], F), "Y": ("sbuf", [128, 4 * W], F), "TM": ("sbuf", [128, 2 * K], F),
    "PL": ("sbuf", [128, 16 * N], U), "LL": ("sbuf", [128, 32], U), "AC": ("sbuf", [128, 2048], F), "IO": ("sbuf", [128, 512], F),
    "NB": ("sbuf", [128, 256], F), "ND": ("dram", [N, 128, 2], F), "SO": ("sbuf", [128, K], F),
    "VI": ("sbuf", [128, 32], I), "VJ": ("sbuf", [128, 32], I), "UL": ("sbuf", [128, 32], U),
    "V2": ("sbuf", [128, 2], I), "CI": ("sbuf", [128, 18], I), "CF": ("sbuf", [128, 64], F),
    "SE": ("sbuf", [128, 4], U), "SD": ("sbuf", [128, 8], U), "D0": ("sbuf", [128, 128], F), "R0": ("sbuf", [128, 80], F),
    "R1": ("sbuf", [128, 24], F), "D8": ("sbuf", [128, 8], F),
}
_EV = ["v", "a", "t", "ld_u", "ld_g0", "ld_g1", "on", "ul", "io1", "io2", "io3", "io4", "io5", "io6", "io7", "mst", "ut", "uq",
       "gq0", "gq1", "ms0", "ms1", "sr", "sco", "sg", "sl", "er0", "xx", "za", "lt", "zw", "zl", "eq", "rks", "px", "lq",
       "ga", "lst", "qc", "df", "erx", "so", "nb", "nd", "ll", "st", "sent", "pls", "hp", "hc", "tm", "c0", "c1", "c2", "c3"]
SEMAPHORES = _EV + ["%s%d" % (e, n) for e in ("mm", "vc", "li", "rk", "ar", "pl") for n in range(N)] \
    + ["%s%d" % (e, n) for e in ("fv", "fa") for n in range(4)]


def tracked(q, T, name):
    tot, pend = {}, {}

    def rec(ins, ev=None):
        e = ev or name
        ins.then_inc(T.sem[e], 1)
        tot[e] = tot.get(e, 0) + 1
        pend[e] = tot[e]

    def sync():
        for e in list(pend):
            q.wait_ge(T.sem[e], pend[e])
        pend.clear()
        return dict(tot)
    return rec, sync


def plan(T, topo, r):
    core = T.cores[r]
    others = [T.cores[(r - d) % N] for d in range(1, N)]
    hs = [c for c in topo.cores_of(core) if c != core and all(topo.may_write(c, d) for d in others)]
    hs.sort(key=lambda c: topo.die(c) == topo.die(core))
    out, i = [], 0
    for c, n in zip([core] + hs, SHARE[r]):
        if n or c == core:
            out.append((c, others[i:i + n]))
        i += n
    return others, out


def transfer(topo, src, cores, mask, sem):
    ids = [DstId(rid=topo.addr(d)[0], pnc=topo.addr(d)[1]) for d in cores]
    return RemoteDMATransfer(dst_ids=ids, dma_engine_mask=mask, remote_sem=sem, srcs=[src], dsts=[src] * len(cores))


def helper_program(g, core, T, topo):
    S = T.sem
    for r in range(N):
        if topo.chip(T.cores[r]) != topo.chip(core):
            continue
        for c, dests in plan(T, topo, r)[1]:
            if c != core:
                continue
            own = slice(K * r, K * r + K)
            mask, ne = topo.mask(core, dests[0]), len(topo.engines(core, dests[0]))
            nin = len(topo.engines(T.cores[r], core)) - len(topo.engines(T.cores[r], dests[0]))
            for sem, src in (("hp", T.RP[:, own]), ("hc", T.RC[:, own].bitcast(dt.uint8))):
                g.wait_ge(S[sem], nin)
                g.remote_dma_fused([transfer(topo, src, dests, mask, S["ar%d" % r])], local_sem=S.sent)
            g.wait_ge(S.sent, 2 * ne)


def rank_program(g, core, T, topo):
    r = T.rank_of(core)
    if r is None:
        return helper_program(g, core, T, topo)
    A, AF = AluOpType, ActivationFunctionType
    v, a, t, sy = g.vector, g.scalar, g.tensor, g.sync
    S = T.sem
    vr, vsync = tracked(v, T, "v")
    ar, async_ = tracked(a, T, "a")
    order = [r] + [s for s in range(N) if s != r]
    turn = {s: n for n, s in enumerate(order)}

    def ts(out, in0, s1, s2, op0, op1=None, ev=None):
        if op1 is None:
            vr(v.tensor_scalar(out, in0, s1, None, op0), ev)
        else:
            vr(v.tensor_scalar(out, in0, s1, s2, op0, op1), ev)

    def tt(out, x, y, op, ev=None):
        vr(v.tensor_tensor(out, x, y, op), ev)

    def iota(out, pattern, base, ev):
        g.iota(out, pattern, base, 0, allow_small_or_imprecise_dtypes=True).then_inc(S[ev], 1)

    sy.dma_start(T.U4[:, 0:4], T.u[:, 0:4]).then_inc(S.ld_u, 16)
    sy.dma_start(T.GR[:, 0:1024], T.gr[:, 0:1024]).then_inc(S.ld_g0, 16)
    a.dma_start(T.GR[:, 1024:2048], T.gr[:, 1024:2048]).then_inc(S.ld_g1, 16)

    g.iota(T.VI[:], [[0, 32]], 0, 1).then_inc(S.io1, 1)
    g.iota(T.V2[:], [[128, 2]], 0, 1).then_inc(S.io2, 1)
    iota(T.D0[:], [[0, 2], [128, 4], [1, 16]], 0, "io3")
    iota(T.R0[:], [[0, 10], [1, 8]], 0, "io4")
    g.wait_ge(S.on, 1)
    g.affine_select(T.MM[:], T.ON[:, 0:516], [[-1, 516]], A.is_equal, 0.0, 3, 4).then_inc(S.mst, 1)
    iota(T.R1[:], [[0, 4], [1, N]], 0, "io5")
    iota(T.D8[:], [[0, 2], [32, 4]], 0, "io7")
    g.wait_ge(S.sr, 2)
    g.affine_select(T.SL[:], T.SR[:], [[0, 4], [-1, 128]], A.is_gt, -1.0, 0, 1).then_inc(S.sl, 1)
    iota(T.IO[:], [[1, 512]], 0, "io6")

    a.wait_ge(S.on, 1)
    for out, n, ev in ((T.WW[:, 0:160], 160, "zw"), (T.WW[:, 512:704], 192, "zw"), (T.TT[:, 352:448], 96, "zw"),
                       (T.ZT[:], 32, "zl"), (T.LQ[:, 16:32], 16, "zl")):
        ar(a.activation(out, T.ON[:, 0:n], AF.Copy, scale=0.0), ev)
    for b in range(4):
        ar(a.activation(T.Y[:, W * b:W * b + 8], T.ON[:, 0:8], AF.Copy, scale=0.0), "zl")
    a.wait_ge(S.ld_u, 16)
    a.wait_ge(S.ul, 1)
    ar(a.activation(T.UT[:], T.U4[:, 0:4].indirect(T.UL[:, 0:32]), AF.Copy), "ut")

    vr(v.memset(T.ON[:], 1.0), "on")
    v.wait_ge(S.io1, 1)
    ts(T.VJ[:], T.VI[:], 3, None, A.bitwise_and)
    vsync()
    vr(v.tensor_copy(T.UL[:], T.VJ[:]), "ul")
    v.wait_ge(S.io2, 1)
    ci = lambda k: T.CI[:, 2 * k:2 * k + 2]
    cf = lambda k: T.CF[:, 2 * k:2 * k + 2]
    ts(ci(0), T.V2[:], 14, None, A.bitwise_and)
    ts(ci(1), T.V2[:], 12, None, A.bitwise_and)
    ts(ci(2), T.V2[:], 1, None, A.bitwise_and)
    ts(ci(3), T.V2[:], 1, 1, A.arith_shift_right, A.bitwise_and)
    ts(ci(4), T.V2[:], 4, 1, A.arith_shift_right, A.bitwise_and)
    ts(ci(5), T.V2[:], 128, None, A.bitwise_and)
    ts(ci(6), T.V2[:], 31, None, A.bitwise_and)
    ts(ci(7), T.V2[:], 112, None, A.bitwise_and)
    vsync()
    vr(v.tensor_copy(T.CF[:, 0:16], T.CI[:, 0:16]))
    vsync()
    tt(cf(8), cf(3), cf(4), A.mult)
    ts(cf(11), cf(1), 8.0, None, A.mult)
    ts(cf(12), cf(2), 16.0, None, A.mult)
    ts(cf(13), cf(3), 192.0, None, A.mult)
    ts(cf(14), cf(4), 160.0, None, A.mult)
    v.wait_ge(S.io3, 1)
    ts(T.DD[:], T.D0[:], T.CF[:, 14:15], None, A.add)
    v.wait_ge(S.io4, 1)
    ts(T.RM[:], T.R0[:], 1.0, None, A.min)
    vsync()
    ts(cf(15), cf(8), 352.0, None, A.mult)
    tt(cf(25), cf(5), cf(11), A.add)
    tt(cf(26), cf(12), cf(13), A.add)
    vsync()
    tt(cf(27), cf(14), cf(15), A.subtract)
    tt(cf(28), cf(25), cf(26), A.add)
    vsync()
    tt(T.SE[:, 0:2], cf(28), cf(27), A.add)

    v.wait_ge(S.ut, 1)
    vr(v.quantize_mx(T.UQ[:], T.UP[:], T.UT[:]), "uq")
    for h in range(2):
        v.wait_ge(S["ld_g%d" % h], 16)
        c = slice(256 * h, 256 * h + 256)
        vr(v.quantize_mx(T.GQ[:, c], T.GP[:, c], T.GR[:, 1024 * h:1024 * h + 1024]), "gq%d" % h)
    v.wait_ge(S.mst, 1)
    for b in range(4):
        vr(v.quantize_mx(T.EQ[:, 128 * b:128 * b + 128], T.EP[:, 128 * b:128 * b + 128], T.MM[:, 3 - b:515 - b]), "eq")
    t.wait_ge(S.uq, 1)
    for h in range(2):
        t.wait_ge(S["gq%d" % h], 1)
        c = slice(256 * h, 256 * h + 256)
        t.matmul_mx(T.PS[:, 512 * h:512 * h + 256], T.UQ[:], T.UP[:], T.GQ[:, c], T.GP[:, c], True, True).then_inc(S["ms%d" % h], 1)
    for b in range(4):
        c = slice(128 * b, 128 * b + 128)
        t.matmul_mx(T.PS[:, 2048 + 512 * b:2176 + 512 * b], T.GQ[:, c], T.GP[:, c], T.UQ[:], T.UP[:], True, True).then_inc(S.t, 1)
    for h in range(2):
        a.wait_ge(S["ms%d" % h], 1)
        ar(a.activation(T.SR[:, 256 * h:256 * h + 256], T.PS[:, 512 * h:512 * h + 256], AF.Abs), "sr")
    a.wait_ge(S.t, 4)
    ar(a.activation(T.SCO[:], T.PS[:, 2048:4096:512], AF.Abs), "sco")
    async_()
    ar(a.activation(T.SN[:], T.SCO[:], AF.Copy, scale=-1.0))
    async_()
    for b in (2, 3):
        ar(a.activation(T.SG[:, 512 * b - 1024:512 * b - 512], T.SR[:], AF.Sign, bias=T.SN[:, b:b + 1]), "sg")
    for k in range(4):
        ar(a.activation(T.ER[:, 512 * k:512 * k + 512], T.GR[:, 512 * k:512 * k + 512], AF.Copy), "er0")

    v.wait_ge(S.sr, 2)
    v.wait_ge(S.sco, 1)

    def before(b):
        z = 640 * b
        s, x = (T.SCO[:, b:b + 1], lambda i, j: T.SR[:, i:j]) if b < 2 else (0.0, lambda i, j: T.SG[:, 512 * b - 1024 + i:512 * b - 1024 + j])
        if b:
            ts(T.CM[:, z:z + 128 * b], x(0, 128 * b), s, None, A.is_ge)
        ts(T.CM[:, z + 128 * b:z + 512], x(128 * b, 512), s, None, A.is_gt)

    def equal(b):
        ts(T.CM[:, 640 * b + 512:640 * b + 640], T.SL[:, 128 * b:128 * b + 128], T.SCO[:, b:b + 1], None, A.is_equal)

    def count(b):
        z = 640 * b
        vr(v.tensor_tensor_scan(T.CN[:, 320 * b:320 * b + 320], T.CM[:, z:z + 320], T.CM[:, z + 320:z + 640], -256.0, A.add, A.add))
    before(0)
    before(1)
    v.wait_ge(S.sl, 1)
    for b in range(4):
        equal(b)
    v.wait_ge(S.sg, 2)
    before(2)
    vsync()
    before(3)
    for b in range(3):
        count(b)
    vsync()
    count(3)
    vsync()

    def permute(val, out, between=None):
        vr(v.tensor_copy(T.WW[:, 0:1056].indirect(T.OFF[:, 0:8]), val))
        vsync()
        if between:
            between()
        vr(v.transpose(T.TT[:, 0:160], T.WW[:, 0:160]))
        vr(v.transpose(T.TT[:, 160:352], T.WW[:, 512:704]))
        vsync()
        vr(v.tensor_copy(T.XX[:], T.TT[:, 0:448].indirect(T.SE[:, 0:2])), "xx")
        n = vsync()["xx"]
        a.wait_ge(S.xx, n)
        vr(v.tensor_copy(T.ZZ[:, 0:80:4], T.XX[:, 0:20]))
        for p in (0, 64):
            vr(v.tensor_copy(T.ZZ[64 - p:128 - p, 2:80:4], T.XX[p:p + 64, 0:20]))
        for d in (1, 3):
            for p in range(4):
                o = 32 * (p ^ d)
                dst, src = T.ZZ[o:o + 32, d:80:4], T.XX[32 * p:32 * p + 32, 0:20]
                if d == 1 and p < 3:
                    vr(v.tensor_copy(dst, src))
                else:
                    ar(a.activation(dst, src, AF.Copy), "za")
        vsync()
        v.wait_ge(S.za, 5 * n)
        vr(v.tensor_tensor_scan(out[:], T.RM[:], T.ZZ[:], 0.0, A.mult, A.add))
        vsync()
        return out[:, 7:80:8]

    rk = T.CN[:, 319:1280:320]
    ts(T.OFF[:, 0:4], rk, 256.0, None, A.add)
    ts(T.OFF[:, 4:8], rk, 784.0, None, A.add)
    ts(T.QM[:], rk, -96.0, None, A.is_lt)
    ts(T.QX[:], rk, float(264 + K * r), None, A.add)
    vsync()
    v.wait_ge(S.zw, 3)
    tt(T.QS[:], T.QM[:], T.QX[:], A.mult)
    num = permute(T.DD[:], T.SC, lambda: ts(T.RK[:, 8 * r:8 * r + 4], T.QS[:], 0.0, None, A.add, ev="rks"))
    for k in (2, 3, 0, 1):
        ts(T.LT[:, L * k:L * k + L], num, 4.0, float(k), A.mult, A.add, ev="lt" if k > 1 else None)

    a.wait_ge(S.lt, 2)
    for k in (2, 3):
        ar(a.activation(T.CG[:, k:4 * K:4], T.GR[:].indirect(T.LT[:, L * k:L * k + L]), AF.Copy), "ga")
    vsync()
    for k in (0, 1):
        vr(v.tensor_copy(T.CG[:, k:4 * K:4], T.GR[:].indirect(T.LT[:, L * k:L * k + L])))
    vsync()
    v.wait_ge(S.ga, 2)
    own = slice(K * r, K * r + K)
    vr(v.quantize_mx(T.RC[:, own], T.RP[:, own], T.CG[:]), "qc")
    ts(T.LP[:, 0:L], num, 0.0, None, A.add, ev="lst")
    ts(T.LP[:, L:16], T.SC[:, 7:55:8], 0.0, None, A.add, ev="lst")

    others, roads = plan(T, topo, r)
    off, ne = topo.mask(core, others[0]), len(topo.engines(core, others[0]))
    hs = [c for c, _ in roads[1:]]
    on = topo.mask(core, hs[0]) & ~off if hs else 0
    n_on = len(topo.engines(core, hs[0])) - ne if hs else 0
    direct = roads[0][1]
    sent = [0]

    def send(trs, n):
        g.remote_dma_fused(trs, local_sem=S.sent)
        sent[0] += n

    def out(src, sem, hsem):
        trs = []
        if hs:
            trs.append(transfer(topo, src, hs, on, S[hsem]))
        if direct:
            trs.append(transfer(topo, src, direct, off, S[sem]))
        send(trs, (n_on if hs else 0) + (ne if direct else 0))
    g.wait_ge(S.rks, 1)
    send([transfer(topo, T.RK[:, 8 * r:8 * r + 4], others, off, S["rk%d" % r])], ne)
    g.wait_ge(S.qc, 1)
    out(T.RP[:, own], "ar%d" % r, "hp")
    out(T.RC[:, own].bitcast(dt.uint8), "ar%d" % r, "hc")

    mixed = lambda s: s not in (0, r)

    def free(n):
        t.wait_ge(S["vc%d" % n], 3 if mixed(order[n]) else 4)
        if mixed(order[n]):
            t.wait_ge(S.c3, order[n])

    def decode(n):
        s = order[n]
        if n == 0:
            t.wait_ge(S.qc, 1)
            t.wait_ge(S.eq, 4)
            t.wait_ge(S.sr, 2)
        else:
            t.wait_ge(S["ar%d" % s], 2 * ne)
            if n == 1:
                t.wait_ge(S.sco, 1)
            else:
                free(n - 2)
        z = 2048 * (n % 2)
        for b in range(4):
            t.matmul_mx(T.PS[:, z + 512 * b:z + 512 * b + K], T.EQ[:, 128 * b:128 * b + 128], T.EP[:, 128 * b:128 * b + 128],
                        T.RC[:, K * s:K * s + K], T.RP[:, K * s:K * s + K], True, True).then_inc(S["mm%d" % n], 1)

    def unload(n):
        s, z = order[n], 2048 * (n % 2)
        a.wait_ge(S["mm%d" % n], 4)
        for b in range(3 if mixed(s) else 4):
            o = W * b + 8 + K * s
            ar(a.activation(T.Y[:, o:o + K], T.PS[:, z + 512 * b:z + 512 * b + K], AF.Copy), "vc%d" % n)
    for n in range(N):
        decode(n)

    a.wait_ge(S.io6, 1)
    a.wait_ge(S.lst, 2)
    ar(a.activation(T.NB[:], T.IO[:].indirect(T.LP[:]), AF.Copy), "nb")
    ar(a.activation(T.SO[:], T.SR[:].indirect(T.LP[:, 0:L]), AF.Copy), "so")

    ts(cf(9), cf(2), T.CF[:, 8:9], None, A.mult)
    ts(cf(16), cf(0), 0.5, None, A.mult)
    ts(cf(17), cf(5), 0.0625, None, A.mult)
    tt(cf(18), cf(2), cf(4), A.add)
    v.wait_ge(S.io5, 1)
    ts(T.RN[:], T.R1[:], 1.0, None, A.min)
    v.wait_ge(S.io7, 1)
    ts(T.SD[:], T.D8[:], T.CF[:, 12:13], None, A.add)
    vsync()
    ts(cf(19), cf(9), 64.0, None, A.mult)
    ts(cf(20), cf(18), 32.0, None, A.mult)
    tt(cf(21), cf(16), cf(17), A.add)
    vsync()
    tt(cf(22), cf(20), cf(19), A.subtract)
    vsync()
    tt(T.SE[:, 2:4], cf(21), cf(22), A.add)

    v.wait_ge(S.mm0, 4)
    for b in range(4):
        tt(T.DF[:, K * b:K * b + K], T.CG[:, b:4 * K:4], T.PS[:, 512 * b:512 * b + K], A.subtract, ev="df")
    a.wait_ge(S.df, 4)
    unload(0)

    for s in order[1:]:
        v.wait_ge(S["rk%d" % s], ne)
    for b in range(4):
        vr(v.tensor_copy(T.QV[:, N * b:N * b + N], T.RK[:, b:8 * N:8]))
    vsync()
    vr(v.tensor_tensor_scan(T.PX[:], T.RN[:], T.QV[:], 0.0, A.mult, A.max), "px")
    vsync()
    v.wait_ge(S.zl, 6)
    pl = lambda s: T.PL[:, 16 * s:16 * s + L]
    if r:
        for b in range(4):
            c = N * b + r - 1
            ts(T.EX[:, 32 * b:32 * b + 32], T.ZT[:], T.PX[:, c:c + 1], None, A.add)
        vsync()
        vr(v.transpose(T.ET[:], T.EX[:]))
        vsync()
        vr(v.tensor_copy(T.D2[:], T.ET[:].indirect(T.SD[:, 0:8])))
        vsync()
        ts(pl(r), permute(T.D2[:], T.S2), 0.0, None, A.add, ev="pls")
        g.wait_ge(S.pls, 1)
        send([transfer(topo, pl(r), others, off, S["pl%d" % r])], ne)
    g.wait_ge(S.nd, 16)
    send([transfer(topo, T.ND[r], others, off, S["li%d" % r])], ne)
    a.wait_ge(S.px, 1)
    for p in range(4):
        for d in range(4):
            ar(a.activation(T.LQ[32 * d:32 * d + 32, p:16:4], T.PX[32 * p:32 * p + 32, N - 1:4 * N:N], AF.Copy), "lq")

    vsync()
    v.wait_ge(S.er0, 4)
    vr(v.tensor_copy(T.ER[:].indirect(T.LT[:, 0:40]), T.DF[:]), "erx")
    v.wait_ge(S.lq, 16)
    vr(v.transpose(T.LA[:], T.LQ[:, 0:32]))
    vsync()
    vr(v.tensor_copy(T.LB[:, 0:16], T.LA[:, 16:32]))
    vr(v.tensor_copy(T.LB[:, 16:32], T.LA[:, 0:16]))
    vsync()
    vr(v.transpose(T.LQ[:, 32:64], T.LB[:]))
    vsync()
    vr(v.tensor_copy(T.LL[:], T.LQ[:].indirect(T.SE[:, 2:4])), "ll")
    vsync()

    tm = lambda s: T.TM[:, K * (s % 2):K * (s % 2) + K]
    for n in range(1, N):
        s = order[n]
        unload(n)
        if mixed(s):
            if s == 1 or (s == 2 and r == 1):
                async_()
            a.wait_ge(S["pl%d" % s], ne)
            if s > 1:
                a.wait_ge(S.c3, s - 1)
            ar(a.activation(tm(s), T.Y[:, 3 * W:3 * W + 8 + K * s].indirect(pl(s)), AF.Copy), "tm")
    nt = 0
    for s in range(1, N):
        if s != r:
            v.wait_ge(S["pl%d" % s], ne)
        for k in ([0, 1] if s == 1 else [s]):
            v.wait_ge(S["vc%d" % turn[k]], 3 if mixed(k) else 4)
        for b in (3, 0, 1, 2):
            o = W * b + 8 + K * s
            if s > 1:
                v.wait_ge(S["c%d" % b], s - 1)
            if b == 3 and mixed(s):
                nt += 1
                v.wait_ge(S.tm, nt)
                z = 2048 * (turn[s] % 2) + 512 * b
                tt(T.Y[:, o:o + K], tm(s), T.PS[:, z:z + K], A.add, ev="c3")
            else:
                tt(T.Y[:, o:o + K], T.Y[:, W * b:o].indirect(pl(s)), T.Y[:, o:o + K], A.add, ev="c%d" % b)

    def lay(b, h):
        return T.AC[:, 512 * h + b:512 * h + 512:4], T.Y[:, W * b:W * b + W].indirect(T.LL[:, 8 * h:8 * h + 8])

    def lay_a(b, h):
        dst, win = lay(b, h)
        ar(a.activation(dst, win, AF.Copy), "fa%d" % h)
    a.wait_ge(S.ll, 1)
    a.wait_ge(S.c3, N - 1)
    for h in range(4):
        lay_a(3, h)
    a.wait_ge(S.c2, N - 1)
    a.wait_ge(S.c1, N - 1)
    v.wait_ge(S.c0, N - 1)
    for h in range(4):
        for b in ((0, 1) if h < 2 else (0,)):
            if h == 0 and b == 1:
                v.wait_ge(S.c1, N - 1)
            dst, win = lay(b, h)
            vr(v.tensor_copy(dst, win), "fv%d" % h)
        for b in ((2,) if h < 2 else (2, 1)):
            lay_a(b, h)
    vsync()

    sy.wait_ge(S.nb, 1)
    sy.dma_start(T.ND[r], T.NB[0:1, :]).then_inc(S.nd, 16)
    sy.dma_start(T.nb[r:r + 1, :], T.NB[0:1, 0:K]).then_inc(S.st, 16)
    sy.wait_ge(S.so, 1)
    sy.dma_start(T.sc[:], T.SO[0:1, :]).then_inc(S.st, 16)
    sy.wait_ge(S.erx, 1)
    sy.dma_start(T.er[:], T.ER[:]).then_inc(S.st, 16)
    for s in order[1:]:
        sy.wait_ge(S["li%d" % s], ne)
        sy.dma_start(T.nb[s:s + 1, :], T.ND[s, 0:K // 2, :]).then_inc(S.st, 16)
    for h in range(4):
        sy.wait_ge(S["fv%d" % h], 2 if h < 2 else 1)
        sy.wait_ge(S["fa%d" % h], 2 if h < 2 else 3)
        sy.dma_start(T.acc[:, 512 * h:512 * h + 512], T.AC[:, 512 * h:512 * h + 512]).then_inc(S.st, 16)
    g.wait_ge(S.sent, sent[0])
    sy.wait_ge(S.st, 16 * (N + 6))
